import numpy as np
import ml_dtypes


def mxq(x, axis, fmt="e4m3"):
    dtype, down = {"e4m3": (ml_dtypes.float8_e4m3fn, 7), "e5m2": (ml_dtypes.float8_e5m2, 14)}[fmt]
    v = np.moveaxis(np.asarray(x, np.float32).astype(ml_dtypes.bfloat16).astype(np.float64), axis, -1)
    blocks = v.reshape(v.shape[:-1] + (-1, 32))
    amax = np.abs(blocks).max(-1, keepdims=True)
    byte = np.maximum(np.where(amax > 0, np.frexp(amax)[1] - 1 + 127, 0) - down, 1)
    scale = np.exp2(byte - 127.0)
    codes = (blocks / scale).astype(np.float32).astype(dtype).astype(np.float64)
    return np.moveaxis((codes * scale).reshape(v.shape), -1, axis)


WIDE = False


def mx_kscale(k):
    if not WIDE:
        return np.ones(k)
    levels = np.array([10, -10, 5, -5, 0])
    if k % 512:
        return np.exp2(np.random.permutation(np.resize(levels, k // 32))).repeat(32)
    a = np.empty((k // 512, 16))
    for p in range(k // 512):
        a[p, :8] = np.random.permutation(np.resize(levels, 8))
        for g in range(8):
            far = levels[np.abs(levels - a[p, g]) >= 10]
            a[p, g + 8] = far[np.random.randint(len(far))]
    return np.exp2(a.ravel()).repeat(32)


BF16 = ml_dtypes.bfloat16


def bf(x):
    return np.asarray(x, np.float32).astype(BF16)


def f64(x):
    return np.asarray(x).astype(np.float64)


E2M1 = np.array([0.0, 0.5, 1.0, 1.5, 2.0, 3.0, 4.0, 6.0, -0.0, -0.5, -1.0, -1.5, -2.0, -3.0, -4.0, -6.0])


def pack_weight(w, fmt):
    k, n = w.shape
    w = f64(bf(w)).reshape(k // 32, 32, n)
    amax = np.abs(w).max(1)
    if fmt == "e4m3":
        byte = np.frexp(amax)[1] - 1 + 127 - 7
    else:
        mant, ex = np.frexp(amax / 6.0)
        byte = np.where(mant > 0.5, ex, ex - 1) + 127
    byte = np.clip(np.where(amax > 0, byte, 1), 1, 254)
    scaled = (w * np.exp2(127.0 - byte)[:, None, :]).reshape(k, n).astype(np.float32)
    by_word = np.ascontiguousarray(scaled.reshape(k // 512, 128, 4, n).transpose(0, 1, 3, 2))
    if fmt == "e4m3":
        words = by_word.astype(ml_dtypes.float8_e4m3fn).view(np.uint8)
    else:
        c = by_word.astype(ml_dtypes.float4_e2m1fn).view(np.uint8) & 0xF
        words = c[..., 0::2] | (c[..., 1::2] << 4)
    return np.ascontiguousarray(words), np.ascontiguousarray(byte.astype(np.uint8).reshape(k // 512, 16, n))


def unpack_weight(words, scales, fmt):
    g, p, n, _ = words.shape
    if fmt == "e4m3":
        vals = np.ascontiguousarray(words).view(ml_dtypes.float8_e4m3fn).astype(np.float64)
    else:
        nib = np.empty((g, p, n, 4), np.uint8)
        nib[..., 0::2] = words & 0xF
        nib[..., 1::2] = words >> 4
        vals = E2M1[nib]
    vals = vals * np.repeat(np.exp2(scales.astype(np.float64) - 127.0), 8, axis=1)[..., None]
    return vals.transpose(0, 1, 3, 2).reshape(g * 512, n)
def pack4(w):
    words, scales = pack_weight(w, "e2m1")
    return words.reshape(words.shape[0], 128, -1), scales


def unpack4(words, scales):
    return unpack_weight(words.reshape(words.shape[0], 128, -1, 2), scales, "e2m1")


A, E, F = 1024, 2048, 1024


def setup_inputs():
    s, u, t = mx_kscale(E), mx_kscale(F), mx_kscale(A)
    e_size = (E * E * A) ** 0.125
    f_size = (F * F * A) ** 0.125
    rw, rs = pack4(np.random.standard_normal((E, A)) / e_size * s[:, None])
    lw, ls = pack4(np.random.standard_normal((E, A)) / e_size / s[:, None] * t)
    return {"ref_ket_words": rw, "ref_ket_scales": rs,
            "ref_bra_words": lw, "ref_bra_scales": ls,
            "ket": bf(np.random.standard_normal((A, F)) / f_size * u / t[:, None]),
            "bra": bf(np.random.standard_normal((A, F)) / f_size / u),
            "filt": bf(1 + 0.1 * np.random.standard_normal(A)),
            "coh": bf(np.random.uniform(0.2, 1.0, (A, A)))}


def reference(ref_ket_words, ref_ket_scales, ref_bra_words, ref_bra_scales, ket, bra, filt, coh):
    r = unpack4(ref_ket_words, ref_ket_scales)
    l = unpack4(ref_bra_words, ref_bra_scales)
    rho = r.T @ l
    rho = rho * f64(filt)[None, :]
    sigma = mxq(f64(ket), 1, "e4m3") @ mxq(f64(bra), 1, "e4m3").T
    sigma = sigma * f64(coh)
    return mxq(rho, 1, "e4m3") @ mxq(sigma, 0, "e4m3")

@@ -1,0 +1,426 @@
+from contextlib import ExitStack
+
+import concourse.mybir as mybir
+from concourse.masks import make_identity
+
+F32 = mybir.dt.float32
+BF16 = mybir.dt.bfloat16
+I32 = mybir.dt.int32
+U32 = mybir.dt.uint32
+U8 = mybir.dt.uint8
+FP8X4 = mybir.dt.float8_e4m3fn_x4
+FP4X4 = mybir.dt.float4_e2m1fn_x4
+MULT = mybir.AluOpType.mult
+COPY = mybir.ActivationFunctionType.Copy
+
+A, E, F = 1024, 2048, 1024
+FLOPS = 2 * A * A * (E + F + A)
+P = 128
+HALF = 512
+
+
+def tile_two_copy_overlap_s12_kernel(
+    tc, ref_ket_words, ref_ket_scales, ref_bra_words, ref_bra_scales, ket, bra, filt, coh, out
+):
+    nc = tc.nc
+    with ExitStack() as ctx:
+        keep = ctx.enter_context(tc.tile_pool(name="keep", bufs=1))
+        stage = ctx.enter_context(tc.tile_pool(name="stage", bufs=2))
+        psum = ctx.enter_context(tc.psum_pool(name="psum", bufs=1))
+        ctx.enter_context(tc.manual_schedule())
+
+        def kept(name, shape, dtype):
+            return keep.tile(shape, dtype, name=name, align_bytes=64)
+
+        banks = [psum.tile([P, HALF], F32, name="bank%d" % b) for b in range(8)]
+        turn = [0]
+
+        def next_bank():
+            turn[0] += 1
+            return banks[(turn[0] - 1) % 8]
+
+        ident = kept("ident", [P, P], F32)
+        perm = kept("perm", [P, P], F32)
+        tiny = kept("tiny", [P, 16], F32)
+        filt_raw = kept("filt_raw", [P, 2, 16], BF16)
+        filt_col = kept("filt_col", [P, 2, 4], F32)
+        rows = {(w, j): kept("%s_rows%d" % (w, j), [P, F], BF16) for w in ("ket", "bra") for j in range(8)}
+        turned = {(w, g): kept("%s_turned%d" % (w, g), [P, 2, HALF * 4], BF16) for w in ("ket", "bra") for g in range(2)}
+        codes = {(w, g): kept("%s_codes%d" % (w, g), [P, 2, HALF], U32) for w in ("ket", "bra") for g in range(2)}
+        scales = {(w, g): kept("%s_scales%d" % (w, g), [P, 2, HALF], U8) for w in ("ket", "bra") for g in range(2)}
+        l_raw = [kept("l_raw%d" % g, [P, 4, 2 * HALF], U8) for g in range(2)]
+        l_words = [kept("l_words%d" % g, [P, 4, 4, 2 * P], U8) for g in range(2)]
+        l_scale_raw = [kept("l_scale_raw%d" % g, [P, 4, HALF], U8) for g in range(2)]
+        l_scale = [kept("l_scale%d" % g, [P, 4, 4, P], U8) for g in range(2)]
+        r_words = [kept("r_words%d" % h, [P, 4, 2 * HALF], U8) for h in range(2)]
+        r_scale = [kept("r_scale%d" % h, [P, 4, HALF], U8) for h in range(2)]
+        coh_sb = {(g, ch): kept("coh%d%d" % (g, ch), [P, 4, HALF], BF16) for g in range(2) for ch in range(2)}
+        q_codes = {(w, g, h): kept("%s_q%d%d" % (w, g, h), [P, HALF], U32) for w in ("rho", "sig") for g in range(2) for h in range(2)}
+        q_scales = {(w, g, h): kept("%s_s%d%d" % (w, g, h), [P, HALF], U8) for w in ("rho", "sig") for g in range(2) for h in range(2)}
+        flat = {}
+        woven = {}
+
+        def load_rows(w, j):
+            src = ket if w == "ket" else bra
+            nc.sync.dma_start(out=rows[w, j][:], in_=src[j * P : (j + 1) * P, :])
+
+        def load_scales(plane, src, h):
+            by_row = src.bitcast(I32).rearrange("e (q r) n -> r q e n", r=4)
+            for r in range(4):
+                nc.sync.dma_start(out=plane[r:P:32, :, :].bitcast(I32), in_=by_row[r][:, :, h * P : (h + 1) * P])
+
+        def load_words(tile, src, h, e0, e1, queue=nc.sync):
+            view = src.bitcast(I32).rearrange("e p n -> p e n")
+            queue.dma_start(out=tile[:, e0:e1, :].bitcast(I32), in_=view[:, e0:e1, h * 256 : (h + 1) * 256])
+
+        def load_coh(g, ch):
+            view = coh.rearrange("(g p t j) c -> g j p t c", g=2, t=4, j=4)
+            for j in range(4):
+                nc.sync.dma_start(out=coh_sb[g, ch][j:P:4, :, :], in_=view[g][j][:, :, ch * HALF : (ch + 1) * HALF])
+
+        def zero(engine, plane):
+            engine.memset(plane[:].rearrange("p e n -> p (e n)").bitcast(I32), 0)
+
+        ordered = {}
+        turned_bank = {}
+
+        def copy_on(engine, out, in_):
+            if engine == "act":
+                nc.scalar.copy(out=out, in_=in_)
+            else:
+                nc.vector.tensor_copy(out=out, in_=in_)
+
+        def order_rows(w, j, engine):
+            ordered[w, j] = stage.tile([P, HALF], F32, name="ordered", bufs=6, align_bytes=64)
+            copy_on(
+                engine,
+                ordered[w, j][:].rearrange("k (h u p) -> k h u p", h=2, u=2),
+                rows[w, j][:].bitcast(F32).rearrange("k (h p u) -> k h u p", h=2, u=2),
+            )
+
+        def turn_mm(w, j):
+            bank = next_bank()
+            turned_bank[w, j] = bank
+            words = rows[w, j][:].bitcast(F32)
+            for u in range(2):
+                for h in range(2):
+                    if (w, j) in ordered:
+                        src = ordered[w, j][:, 256 * h + P * u : 256 * h + P * (u + 1)]
+                    else:
+                        src = words[:, 256 * h + u : 256 * (h + 1) : 2]
+                    nc.tensor.transpose(
+                        bank[:, 256 * u + P * h : 256 * u + P * (h + 1)], src, (perm if w == "ket" else ident)[:]
+                    )
+
+        def turn_out(w, j, engine):
+            bank = turned_bank[w, j]
+            dst = turned[w, j // 4][:].rearrange("p h x -> p (h x)").bitcast(F32)
+            jj = j % 4
+            if w == "ket":
+                copy_on(
+                    engine,
+                    dst.rearrange("p (s jj c u) -> p jj s c u", s=8, jj=4, u=2)[:, jj],
+                    bank[:].rearrange("p (u s c) -> p s c u", u=2, s=8),
+                )
+            else:
+                copy_on(
+                    engine,
+                    dst.rearrange("p (h jj c u) -> p jj h c u", h=2, jj=4, u=2)[:, jj],
+                    bank[:].rearrange("p (u h c) -> p h c u", u=2, h=2),
+                )
+
+        def turn_rows(w, j, engine="act"):
+            turn_mm(w, j)
+            turn_out(w, j, engine)
+
+        def quant_turned(w, g, h, c0, c1):
+            nc.vector.quantize_mx(
+                out=codes[w, g][:, h, c0:c1].bitcast(FP8X4),
+                scales=scales[w, g][:, h, c0:c1],
+                in_=turned[w, g][:, h, 4 * c0 : 4 * c1],
+            )
+
+        def order_l_scales(g):
+            nc.vector.tensor_copy(
+                out=l_scale[g][:].rearrange("k t e n -> k t (e n)").bitcast(I32),
+                in_=l_scale_raw[g][:].rearrange("k e n -> k (e n)").bitcast(I32).rearrange("k (x t) -> k t x", t=4),
+            )
+
+        def order_l_words(g, e0, e1):
+            nc.vector.tensor_copy(
+                out=l_words[g][:, :, e0:e1, :].rearrange("k t e n -> k t (e n)").bitcast(I32).rearrange("k t (x w) -> k t x w", w=2),
+                in_=l_raw[g][:, e0:e1, :].rearrange("k e n -> k (e n)").bitcast(I32).rearrange("k (x t w) -> k t x w", t=4, w=2),
+            )
+
+        def rho_pass(bank, g, ah, t, e):
+            nc.tensor.matmul_mx(
+                out=bank[:],
+                lhsT=l_words[g][:, t, e, :].bitcast(FP4X4),
+                lhsT_scale=l_scale[g][:, t, e, :],
+                rhs=r_words[ah][:, e, :].bitcast(FP4X4),
+                rhs_scale=r_scale[ah][:, e, :],
+                start=(e == 0),
+                stop=(e == 3),
+            )
+
+        def rho_out(bank, g, ah, t):
+            if t == 0:
+                flat["rho", g, ah] = stage.tile([P, 4, HALF], BF16, name="rho_flat", align_bytes=64)
+            nc.scalar.activation(out=flat["rho", g, ah][:, t, :], in_=bank[:], func=COPY, scale=filt_col[:, g, t : t + 1])
+
+        def rho_group(g, ah, t):
+            bank = next_bank()
+            for e in range(4):
+                rho_pass(bank, g, ah, t, e)
+            rho_out(bank, g, ah, t)
+
+        def weave_rho(g, ah, c0=0, c1=HALF):
+            if c0 == 0:
+                woven["rho", g, ah] = stage.tile([P, HALF * 4], BF16, name="woven", bufs=3, align_bytes=64)
+            nc.vector.tensor_copy(
+                out=woven["rho", g, ah][:, 4 * c0 : 4 * c1].rearrange("p (c i t) -> p c t i", i=4, t=4),
+                in_=flat["rho", g, ah][:, :, c0:c1].rearrange("p t (c i) -> p c t i", i=4),
+            )
+
+        def quant_woven(w, g, h, c0=0, c1=HALF):
+            nc.vector.quantize_mx(
+                out=q_codes[w, g, h][:, c0:c1].bitcast(FP8X4),
+                scales=q_scales[w, g, h][:, c0:c1],
+                in_=woven[w, g, h][:, 4 * c0 : 4 * c1],
+            )
+
+        held = {}
+
+        def sig_mm(g, ch, cq, tp):
+            bank = next_bank()
+            held[g, ch, cq, tp] = bank
+            cols = slice(256 * cq, 256 * (cq + 1))
+            for tt in range(2):
+                m_cols = slice(P * (2 * tp + tt), P * (2 * tp + tt + 1))
+                for h in range(2):
+                    nc.tensor.matmul_mx(
+                        out=bank[:, 256 * tt : 256 * (tt + 1)],
+                        lhsT=codes["ket", g][:, h, m_cols].bitcast(FP8X4),
+                        lhsT_scale=scales["ket", g][:, h, m_cols],
+                        rhs=codes["bra", ch][:, h, cols].bitcast(FP8X4),
+                        rhs_scale=scales["bra", ch][:, h, cols],
+                        start=(h == 0),
+                        stop=(h == 1),
+                    )
+
+        def sig_out(g, ch, cq, tp):
+            if cq == 0 and tp == 0:
+                flat["sig", g, ch] = stage.tile([P, 2, HALF, 2], BF16, name="sig_pairs", align_bytes=64)
+            cols = slice(256 * cq, 256 * (cq + 1))
+            nc.vector.tensor_tensor(
+                out=flat["sig", g, ch][:, tp, cols, :],
+                in0=held[g, ch, cq, tp][:].rearrange("p (tt c) -> p c tt", tt=2),
+                in1=coh_sb[g, ch][:, 2 * tp : 2 * tp + 2, cols].rearrange("p tt c -> p c tt"),
+                op=MULT,
+            )
+
+        def sig_group(g, ch, cq, tp):
+            sig_mm(g, ch, cq, tp)
+            sig_out(g, ch, cq, tp)
+
+        def weave_sig(g, ch):
+            woven["sig", g, ch] = stage.tile([P, HALF * 4], BF16, name="woven", bufs=3, align_bytes=64)
+            nc.vector.tensor_copy(
+                out=woven["sig", g, ch][:].rearrange("p (c tp tt) -> p c tp tt", tp=2, tt=2),
+                in_=flat["sig", g, ch][:].rearrange("p tp c tt -> p c tp tt"),
+            )
+
+        def warm_up(count):
+            blank = kept("blank", [P, HALF], BF16)
+            blank_codes = kept("blank_codes", [P, P], U32)
+            blank_scales = kept("blank_scales", [P, P], U8)
+            nc.vector.memset(blank[:], 0.0)
+            nc.vector.quantize_mx(out=blank_codes[:].bitcast(FP8X4), scales=blank_scales[:], in_=blank[:])
+            for i in range(count):
+                nc.tensor.matmul_mx(
+                    out=banks[7][:, P * (i % 4) : P * (i % 4 + 1)],
+                    lhsT=blank_codes[:].bitcast(FP8X4),
+                    lhsT_scale=blank_scales[:],
+                    rhs=blank_codes[:].bitcast(FP8X4),
+                    rhs_scale=blank_scales[:],
+                    start=True,
+                    stop=True,
+                )
+
+        def out_group(ah, ch, i, engine):
+            bank = next_bank()
+            a_cols = slice(P * i, P * (i + 1))
+            for g in range(2):
+                nc.tensor.matmul_mx(
+                    out=bank[:],
+                    lhsT=q_codes["rho", g, ah][:, a_cols].bitcast(FP8X4),
+                    lhsT_scale=q_scales["rho", g, ah][:, a_cols],
+                    rhs=q_codes["sig", g, ch][:].bitcast(FP8X4),
+                    rhs_scale=q_scales["sig", g, ch][:],
+                    start=(g == 0),
+                    stop=(g == 1),
+                )
+            result = stage.tile([P, HALF], F32, name="result", bufs=8, align_bytes=64)
+            copy_on(engine, result[:], bank[:])
+            row0 = HALF * ah + P * i
+            nc.sync.dma_start(out=out[row0 : row0 + P, HALF * ch : HALF * (ch + 1)], in_=result[:])
+
+        def out_half(ah, ch, i, cq, engine):
+            bank = next_bank()
+            a_cols = slice(P * i, P * (i + 1))
+            cols = slice(256 * cq, 256 * (cq + 1))
+            for g in range(2):
+                nc.tensor.matmul_mx(
+                    out=bank[:, 0:256],
+                    lhsT=q_codes["rho", g, ah][:, a_cols].bitcast(FP8X4),
+                    lhsT_scale=q_scales["rho", g, ah][:, a_cols],
+                    rhs=q_codes["sig", g, ch][:, cols].bitcast(FP8X4),
+                    rhs_scale=q_scales["sig", g, ch][:, cols],
+                    start=(g == 0),
+                    stop=(g == 1),
+                )
+            result = stage.tile([P, 256], F32, name="result", bufs=8, align_bytes=64)
+            copy_on(engine, result[:], bank[:, 0:256])
+            row0 = HALF * ah + P * i
+            col0 = HALF * ch + 256 * cq
+            nc.sync.dma_start(out=out[row0 : row0 + P, col0 : col0 + 256], in_=result[:])
+
+
+        load_words(l_raw[0], ref_bra_words, 0, 0, 2, nc.gpsimd)
+        load_words(r_words[0], ref_ket_words, 0, 0, 2, nc.gpsimd)
+        zero(nc.vector, l_scale_raw[0])
+        zero(nc.vector, r_scale[0])
+        warm_up(18)
+        nc.vector.memset(tiny[:], 0.0)
+        nc.scalar.activation(out=tiny[:, 8:9], in_=tiny[:, 0:1], func=COPY, scale=tiny[:, 1:2])
+        zero(nc.vector, l_scale_raw[1])
+        zero(nc.vector, r_scale[1])
+        make_identity(nc, ident[:])
+        by_16 = filt.rearrange("(g p s) -> p g s", g=2, s=16)
+        for j in range(4):
+            nc.gpsimd.dma_start(out=filt_raw[j:P:4, :, 0:13], in_=by_16[:, :, j : j + 13])
+
+        load_scales(l_scale_raw[0], ref_bra_scales, 0)
+        load_scales(r_scale[0], ref_ket_scales, 0)
+        load_words(l_raw[0], ref_bra_words, 0, 2, 4)
+        load_words(r_words[0], ref_ket_words, 0, 2, 4)
+        load_scales(l_scale_raw[1], ref_bra_scales, 1)
+        load_words(l_raw[1], ref_bra_words, 1, 0, 4)
+        for j in range(4):
+            load_rows("ket", j)
+        for j in range(4):
+            load_rows("bra", j)
+        load_scales(r_scale[1], ref_ket_scales, 1)
+        load_words(r_words[1], ref_ket_words, 1, 0, 4)
+        load_coh(0, 0)
+        for j in range(4, 8):
+            load_rows("ket", j)
+        load_coh(1, 0)
+        for j in range(4, 8):
+            load_rows("bra", j)
+        load_coh(0, 1)
+        load_coh(1, 1)
+
+        order_l_words(0, 0, 2)
+        order_l_scales(0)
+        order_l_words(0, 2, 4)
+        nc.vector.tensor_copy(
+            out=perm[:].rearrange("k (t p j) -> k t p j", t=4, j=4), in_=ident[:].rearrange("k (p t j) -> k t p j", t=4, j=4)
+        )
+        nc.scalar.copy(out=filt_col[:], in_=filt_raw[:, :, 0:13:4])
+        first = [next_bank() for t in range(4)]
+        for e in range(2):
+            for t in range(4):
+                rho_pass(first[t], 0, 0, t, e)
+        for t in range(4):
+            for e in range(2, 4):
+                rho_pass(first[t], 0, 0, t, e)
+            rho_out(first[t], 0, 0, t)
+        order_l_scales(1)
+        order_l_words(1, 0, 4)
+        for j in range(4):
+            order_rows("ket", j, "dve")
+        rho_group(1, 0, 0)
+        rho_group(1, 0, 1)
+        for j in range(4):
+            turn_rows("ket", j, "act")
+        weave_rho(0, 0)
+        for j in range(4):
+            order_rows("bra", j, "dve")
+        rho_group(1, 0, 2)
+        quant_woven("rho", 0, 0)
+        quant_turned("ket", 0, 0, 0, HALF)
+        quant_turned("ket", 0, 1, 0, HALF)
+        for j in range(4):
+            turn_rows("bra", j, "act")
+            if j % 2:
+                quant_turned("bra", 0, 0, P * (j - 1), P * (j + 1))
+                quant_turned("bra", 0, 1, P * (j - 1), P * (j + 1))
+        rho_group(1, 0, 3)
+        rho_group(0, 1, 0)
+        for j in range(4, 8):
+            order_rows("ket", j, "dve" if j < 6 else "act")
+        sig_group(0, 0, 0, 0)
+        sig_group(0, 0, 0, 1)
+        sig_group(0, 0, 1, 0)
+        sig_group(0, 0, 1, 1)
+        for j in range(4, 8):
+            if j == 7:
+                weave_sig(0, 0)
+            turn_rows("ket", j, "act" if j < 7 else "dve")
+        rho_group(0, 1, 1)
+        quant_turned("ket", 1, 0, 0, HALF)
+        quant_turned("ket", 1, 1, 0, HALF)
+        weave_rho(1, 0)
+        rho_group(0, 1, 2)
+        for j in range(4, 8):
+            order_rows("bra", j, "act")
+        sig_group(1, 0, 0, 0)
+        sig_group(1, 0, 0, 1)
+        quant_woven("rho", 1, 0)
+        sig_group(1, 0, 1, 0)
+        sig_group(1, 0, 1, 1)
+        quant_woven("sig", 0, 0)
+        weave_sig(1, 0)
+        for j in range(4, 8):
+            turn_rows("bra", j, "act")
+            if j == 5:
+                quant_turned("bra", 1, 0, 0, 256)
+                quant_turned("bra", 1, 1, 0, 256)
+                quant_woven("sig", 1, 0)
+            if j == 7:
+                quant_turned("bra", 1, 0, 256, HALF)
+                quant_turned("bra", 1, 1, 256, HALF)
+        rho_group(0, 1, 3)
+        rho_group(1, 1, 0)
+        for i in range(4):
+            sig_group(0, 1, i // 2, i % 2)
+        weave_rho(0, 1)
+        for i in range(4):
+            out_group(0, 0, i, "act")
+        weave_sig(0, 1)
+        for i in range(4):
+            sig_group(1, 1, i // 2, i % 2)
+            if i == 0:
+                quant_woven("sig", 0, 1)
+        weave_sig(1, 1)
+        quant_woven("rho", 0, 1)
+        quant_woven("sig", 1, 1)
+        rho_group(1, 1, 1)
+        rho_group(1, 1, 2)
+        rho_group(1, 1, 3)
+        weave_rho(1, 1, 0, 128)
+        weave_rho(1, 1, 128, 256)
+        quant_woven("rho", 1, 1, 0, 128)
+        weave_rho(1, 1, 256, HALF)
+        quant_woven("rho", 1, 1, 128, 256)
+        quant_woven("rho", 1, 1, 256, HALF)
+        for i in range(4):
+            out_group(0, 1, i, "act")
+        for i in range(4):
+            for ch in range(2):
+                if i == 3 and ch == 1:
+                    out_half(1, 1, 3, 0, "act")
+                    out_half(1, 1, 3, 1, "dve")
+                else:
+                    out_group(1, ch, i, "dve" if ch == 0 else "act")

@@ -33,11 +33,11 @@ def tile_two_copy_overlap_s12_kernel(
             return keep.tile(shape, dtype, name=name, align_bytes=64)
 
         banks = [psum.tile([P, HALF], F32, name="bank%d" % b) for b in range(8)]
-        turn = [0]
+        used = [0]
 
         def next_bank():
-            turn[0] += 1
-            return banks[(turn[0] - 1) % 8]
+            used[0] += 1
+            return banks[(used[0] - 1) % 8]
 
         ident = kept("ident", [P, P], F32)
         perm = kept("perm", [P, P], F32)
@@ -45,9 +45,9 @@ def tile_two_copy_overlap_s12_kernel(
         filt_raw = kept("filt_raw", [P, 2, 16], BF16)
         filt_col = kept("filt_col", [P, 2, 4], F32)
         rows = {(w, j): kept("%s_rows%d" % (w, j), [P, F], BF16) for w in ("ket", "bra") for j in range(8)}
-        turned = {(w, g): kept("%s_turned%d" % (w, g), [P, 2, HALF * 4], BF16) for w in ("ket", "bra") for g in range(2)}
-        codes = {(w, g): kept("%s_codes%d" % (w, g), [P, 2, HALF], U32) for w in ("ket", "bra") for g in range(2)}
-        scales = {(w, g): kept("%s_scales%d" % (w, g), [P, 2, HALF], U8) for w in ("ket", "bra") for g in range(2)}
+        turned = {(w, g): kept("%s_turned%d" % (w, g), [P, 2 * HALF * 4], BF16) for w in ("ket", "bra") for g in range(2)}
+        codes = {(w, g): kept("%s_codes%d" % (w, g), [P, 2 * HALF], U32) for w in ("ket", "bra") for g in range(2)}
+        scales = {(w, g): kept("%s_scales%d" % (w, g), [P, 2 * HALF], U8) for w in ("ket", "bra") for g in range(2)}
         l_raw = [kept("l_raw%d" % g, [P, 4, 2 * HALF], U8) for g in range(2)]
         l_words = [kept("l_words%d" % g, [P, 4, 4, 2 * P], U8) for g in range(2)]
         l_scale_raw = [kept("l_scale_raw%d" % g, [P, 4, HALF], U8) for g in range(2)]
@@ -91,7 +91,7 @@ def tile_two_copy_overlap_s12_kernel(
                 nc.vector.tensor_copy(out=out, in_=in_)
 
         def order_rows(w, j, engine):
-            ordered[w, j] = stage.tile([P, HALF], F32, name="ordered", bufs=6, align_bytes=64)
+            ordered[w, j] = stage.tile([P, HALF], F32, name="ordered", bufs=8, align_bytes=64)
             copy_on(
                 engine,
                 ordered[w, j][:].rearrange("k (h u p) -> k h u p", h=2, u=2),
@@ -114,7 +114,7 @@ def tile_two_copy_overlap_s12_kernel(
 
         def turn_out(w, j, engine):
             bank = turned_bank[w, j]
-            dst = turned[w, j // 4][:].rearrange("p h x -> p (h x)").bitcast(F32)
+            dst = turned[w, j // 4][:].bitcast(F32)
             jj = j % 4
             if w == "ket":
                 copy_on(
@@ -129,15 +129,11 @@ def tile_two_copy_overlap_s12_kernel(
                     bank[:].rearrange("p (u h c) -> p h c u", u=2, h=2),
                 )
 
-        def turn_rows(w, j, engine="act"):
-            turn_mm(w, j)
-            turn_out(w, j, engine)
-
-        def quant_turned(w, g, h, c0, c1):
+        def quant_turned(w, g, c0, c1):
             nc.vector.quantize_mx(
-                out=codes[w, g][:, h, c0:c1].bitcast(FP8X4),
-                scales=scales[w, g][:, h, c0:c1],
-                in_=turned[w, g][:, h, 4 * c0 : 4 * c1],
+                out=codes[w, g][:, c0:c1].bitcast(FP8X4),
+                scales=scales[w, g][:, c0:c1],
+                in_=turned[w, g][:, 4 * c0 : 4 * c1],
             )
 
         def order_l_scales(g):
@@ -163,23 +159,26 @@ def tile_two_copy_overlap_s12_kernel(
                 stop=(e == 3),
             )
 
-        def rho_out(bank, g, ah, t):
+        held = {}
+
+        def rho_mm(g, ah, t):
+            held["rho", g, ah, t] = next_bank()
+            for e in range(4):
+                rho_pass(held["rho", g, ah, t], g, ah, t, e)
+
+        def rho_out(g, ah, t):
+            bank = held["rho", g, ah, t]
             if t == 0:
-                flat["rho", g, ah] = stage.tile([P, 4, HALF], BF16, name="rho_flat", align_bytes=64)
+                flat["rho", g, ah] = stage.tile([P, 4, HALF], BF16, name="rho_flat", bufs=3, align_bytes=64)
             nc.scalar.activation(out=flat["rho", g, ah][:, t, :], in_=bank[:], func=COPY, scale=filt_col[:, g, t : t + 1])
 
-        def rho_group(g, ah, t):
-            bank = next_bank()
-            for e in range(4):
-                rho_pass(bank, g, ah, t, e)
-            rho_out(bank, g, ah, t)
-
-        def weave_rho(g, ah, c0=0, c1=HALF):
+        def weave(w, g, ah, c0=0, c1=HALF, engine="dve"):
             if c0 == 0:
-                woven["rho", g, ah] = stage.tile([P, HALF * 4], BF16, name="woven", bufs=3, align_bytes=64)
-            nc.vector.tensor_copy(
-                out=woven["rho", g, ah][:, 4 * c0 : 4 * c1].rearrange("p (c i t) -> p c t i", i=4, t=4),
-                in_=flat["rho", g, ah][:, :, c0:c1].rearrange("p t (c i) -> p c t i", i=4),
+                woven[w, g, ah] = stage.tile([P, HALF * 4], BF16, name="woven", bufs=4, align_bytes=64)
+            copy_on(
+                engine,
+                woven[w, g, ah][:, 4 * c0 : 4 * c1].rearrange("p (c i t) -> p c t i", i=4, t=4),
+                flat[w, g, ah][:, :, c0:c1].rearrange("p t (c i) -> p c t i", i=4),
             )
 
         def quant_woven(w, g, h, c0=0, c1=HALF):
@@ -189,46 +188,27 @@ def tile_two_copy_overlap_s12_kernel(
                 in_=woven[w, g, h][:, 4 * c0 : 4 * c1],
             )
 
-        held = {}
-
-        def sig_mm(g, ch, cq, tp):
+        def sig_mm(g, ch, t):
             bank = next_bank()
-            held[g, ch, cq, tp] = bank
-            cols = slice(256 * cq, 256 * (cq + 1))
-            for tt in range(2):
-                m_cols = slice(P * (2 * tp + tt), P * (2 * tp + tt + 1))
-                for h in range(2):
-                    nc.tensor.matmul_mx(
-                        out=bank[:, 256 * tt : 256 * (tt + 1)],
-                        lhsT=codes["ket", g][:, h, m_cols].bitcast(FP8X4),
-                        lhsT_scale=scales["ket", g][:, h, m_cols],
-                        rhs=codes["bra", ch][:, h, cols].bitcast(FP8X4),
-                        rhs_scale=scales["bra", ch][:, h, cols],
-                        start=(h == 0),
-                        stop=(h == 1),
-                    )
+            held["sig", g, ch, t] = bank
+            for h in range(2):
+                m_cols = slice(HALF * h + P * t, HALF * h + P * (t + 1))
+                cols = slice(HALF * h, HALF * (h + 1))
+                nc.tensor.matmul_mx(
+                    out=bank[:],
+                    lhsT=codes["ket", g][:, m_cols].bitcast(FP8X4),
+                    lhsT_scale=scales["ket", g][:, m_cols],
+                    rhs=codes["bra", ch][:, cols].bitcast(FP8X4),
+                    rhs_scale=scales["bra", ch][:, cols],
+                    start=(h == 0),
+                    stop=(h == 1),
+                )
 
-        def sig_out(g, ch, cq, tp):
-            if cq == 0 and tp == 0:
-                flat["sig", g, ch] = stage.tile([P, 2, HALF, 2], BF16, name="sig_pairs", align_bytes=64)
-            cols = slice(256 * cq, 256 * (cq + 1))
-            nc.vector.tensor_tensor(
-                out=flat["sig", g, ch][:, tp, cols, :],
-                in0=held[g, ch, cq, tp][:].rearrange("p (tt c) -> p c tt", tt=2),
-                in1=coh_sb[g, ch][:, 2 * tp : 2 * tp + 2, cols].rearrange("p tt c -> p c tt"),
-                op=MULT,
-            )
-
-        def sig_group(g, ch, cq, tp):
-            sig_mm(g, ch, cq, tp)
-            sig_out(g, ch, cq, tp)
-
-        def weave_sig(g, ch):
-            woven["sig", g, ch] = stage.tile([P, HALF * 4], BF16, name="woven", bufs=3, align_bytes=64)
-            nc.vector.tensor_copy(
-                out=woven["sig", g, ch][:].rearrange("p (c tp tt) -> p c tp tt", tp=2, tt=2),
-                in_=flat["sig", g, ch][:].rearrange("p tp c tt -> p c tp tt"),
-            )
+        def sig_out(g, ch, t):
+            bank = held["sig", g, ch, t]
+            if t == 0:
+                flat["sig", g, ch] = stage.tile([P, 4, HALF], BF16, name="sig_flat", bufs=2, align_bytes=64)
+            nc.vector.tensor_tensor(out=flat["sig", g, ch][:, t, :], in0=bank[:], in1=coh_sb[g, ch][:, t, :], op=MULT)
 
         def warm_up(count):
             blank = kept("blank", [P, HALF], BF16)
@@ -247,77 +227,80 @@ def tile_two_copy_overlap_s12_kernel(
                     stop=True,
                 )
 
-        def out_group(ah, ch, i, engine):
+        def out_mm(ah, ch, i, c0=0, c1=HALF):
             bank = next_bank()
+            held["out", ah, ch, i, c0] = bank
             a_cols = slice(P * i, P * (i + 1))
             for g in range(2):
                 nc.tensor.matmul_mx(
-                    out=bank[:],
+                    out=bank[:, 0 : c1 - c0],
                     lhsT=q_codes["rho", g, ah][:, a_cols].bitcast(FP8X4),
                     lhsT_scale=q_scales["rho", g, ah][:, a_cols],
-                    rhs=q_codes["sig", g, ch][:].bitcast(FP8X4),
-                    rhs_scale=q_scales["sig", g, ch][:],
+                    rhs=q_codes["sig", g, ch][:, c0:c1].bitcast(FP8X4),
+                    rhs_scale=q_scales["sig", g, ch][:, c0:c1],
                     start=(g == 0),
                     stop=(g == 1),
                 )
-            result = stage.tile([P, HALF], F32, name="result", bufs=8, align_bytes=64)
-            copy_on(engine, result[:], bank[:])
+
+        def out_store(engine, ah, ch, i, c0=0, c1=HALF):
+            result = stage.tile([P, c1 - c0], F32, name="result", bufs=8, align_bytes=64)
+            copy_on(engine, result[:], held["out", ah, ch, i, c0][:, 0 : c1 - c0])
             row0 = HALF * ah + P * i
-            nc.sync.dma_start(out=out[row0 : row0 + P, HALF * ch : HALF * (ch + 1)], in_=result[:])
+            nc.sync.dma_start(out=out[row0 : row0 + P, HALF * ch + c0 : HALF * ch + c1], in_=result[:])
 
-        def out_half(ah, ch, i, cq, engine):
-            bank = next_bank()
-            a_cols = slice(P * i, P * (i + 1))
-            cols = slice(256 * cq, 256 * (cq + 1))
-            for g in range(2):
-                nc.tensor.matmul_mx(
-                    out=bank[:, 0:256],
-                    lhsT=q_codes["rho", g, ah][:, a_cols].bitcast(FP8X4),
-                    lhsT_scale=q_scales["rho", g, ah][:, a_cols],
-                    rhs=q_codes["sig", g, ch][:, cols].bitcast(FP8X4),
-                    rhs_scale=q_scales["sig", g, ch][:, cols],
-                    start=(g == 0),
-                    stop=(g == 1),
-                )
-            result = stage.tile([P, 256], F32, name="result", bufs=8, align_bytes=64)
-            copy_on(engine, result[:], bank[:, 0:256])
-            row0 = HALF * ah + P * i
-            col0 = HALF * ch + 256 * cq
-            nc.sync.dma_start(out=out[row0 : row0 + P, col0 : col0 + 256], in_=result[:])
+        def quant_bra(ch, x):
+            for h in range(2):
+                quant_turned("bra", ch, HALF * h + 256 * x, HALF * h + 256 * (x + 1))
+
+        def rho(g, ah, t):
+            rho_mm(g, ah, t)
+            rho_out(g, ah, t)
+
+        def sig(g, ch, t):
+            sig_mm(g, ch, t)
+            sig_out(g, ch, t)
+
+        def turn(w, j, engine):
+            turn_mm(w, j)
+            turn_out(w, j, engine)
+
+        def outg(engine, ah, ch, i, c0=0, c1=HALF):
+            out_mm(ah, ch, i, c0, c1)
+            out_store(engine, ah, ch, i, c0, c1)
 
 
-        load_words(l_raw[0], ref_bra_words, 0, 0, 2, nc.gpsimd)
-        load_words(r_words[0], ref_ket_words, 0, 0, 2, nc.gpsimd)
+        load_words(l_raw[0], ref_bra_words, 0, 0, 2)
+        load_words(r_words[0], ref_ket_words, 0, 0, 2)
+        by_16 = filt.rearrange("(g p s) -> p g s", g=2, s=16)
+        for j in range(4):
+            nc.gpsimd.dma_start(out=filt_raw[j:P:4, :, 0:13], in_=by_16[:, :, j : j + 13])
+        make_identity(nc, ident[:])
         zero(nc.vector, l_scale_raw[0])
         zero(nc.vector, r_scale[0])
         warm_up(18)
         nc.vector.memset(tiny[:], 0.0)
         nc.scalar.activation(out=tiny[:, 8:9], in_=tiny[:, 0:1], func=COPY, scale=tiny[:, 1:2])
-        zero(nc.vector, l_scale_raw[1])
         zero(nc.vector, r_scale[1])
-        make_identity(nc, ident[:])
-        by_16 = filt.rearrange("(g p s) -> p g s", g=2, s=16)
-        for j in range(4):
-            nc.gpsimd.dma_start(out=filt_raw[j:P:4, :, 0:13], in_=by_16[:, :, j : j + 13])
+        zero(nc.vector, l_scale_raw[1])
 
         load_scales(l_scale_raw[0], ref_bra_scales, 0)
         load_scales(r_scale[0], ref_ket_scales, 0)
         load_words(l_raw[0], ref_bra_words, 0, 2, 4)
         load_words(r_words[0], ref_ket_words, 0, 2, 4)
-        load_scales(l_scale_raw[1], ref_bra_scales, 1)
-        load_words(l_raw[1], ref_bra_words, 1, 0, 4)
+        load_scales(r_scale[1], ref_ket_scales, 1)
+        load_words(r_words[1], ref_ket_words, 1, 0, 4)
         for j in range(4):
             load_rows("ket", j)
         for j in range(4):
             load_rows("bra", j)
-        load_scales(r_scale[1], ref_ket_scales, 1)
-        load_words(r_words[1], ref_ket_words, 1, 0, 4)
+        load_scales(l_scale_raw[1], ref_bra_scales, 1)
+        load_words(l_raw[1], ref_bra_words, 1, 0, 4)
         load_coh(0, 0)
         for j in range(4, 8):
             load_rows("ket", j)
-        load_coh(1, 0)
         for j in range(4, 8):
             load_rows("bra", j)
+        load_coh(1, 0)
         load_coh(0, 1)
         load_coh(1, 1)
 
@@ -328,99 +311,91 @@ def tile_two_copy_overlap_s12_kernel(
             out=perm[:].rearrange("k (t p j) -> k t p j", t=4, j=4), in_=ident[:].rearrange("k (p t j) -> k t p j", t=4, j=4)
         )
         nc.scalar.copy(out=filt_col[:], in_=filt_raw[:, :, 0:13:4])
-        first = [next_bank() for t in range(4)]
+        for t in range(4):
+            held["rho", 0, 0, t] = next_bank()
         for e in range(2):
             for t in range(4):
-                rho_pass(first[t], 0, 0, t, e)
+                rho_pass(held["rho", 0, 0, t], 0, 0, t, e)
         for t in range(4):
             for e in range(2, 4):
-                rho_pass(first[t], 0, 0, t, e)
-            rho_out(first[t], 0, 0, t)
-        order_l_scales(1)
-        order_l_words(1, 0, 4)
+                rho_pass(held["rho", 0, 0, t], 0, 0, t, e)
+            rho_out(0, 0, t)
         for j in range(4):
             order_rows("ket", j, "dve")
-        rho_group(1, 0, 0)
-        rho_group(1, 0, 1)
-        for j in range(4):
-            turn_rows("ket", j, "act")
-        weave_rho(0, 0)
+        rho(0, 1, 0)
+        rho(0, 1, 1)
         for j in range(4):
             order_rows("bra", j, "dve")
-        rho_group(1, 0, 2)
-        quant_woven("rho", 0, 0)
-        quant_turned("ket", 0, 0, 0, HALF)
-        quant_turned("ket", 0, 1, 0, HALF)
         for j in range(4):
-            turn_rows("bra", j, "act")
+            turn("ket", j, "dve" if j % 2 else "act")
+        quant_turned("ket", 0, 0, 2 * HALF)
+        for j in range(4):
+            turn("bra", j, "act")
             if j % 2:
-                quant_turned("bra", 0, 0, P * (j - 1), P * (j + 1))
-                quant_turned("bra", 0, 1, P * (j - 1), P * (j + 1))
-        rho_group(1, 0, 3)
-        rho_group(0, 1, 0)
+                quant_bra(0, j // 2)
+        rho(0, 1, 2)
+        order_l_scales(1)
+        rho(0, 1, 3)
+        order_l_words(1, 0, 4)
+        weave("rho", 0, 0, 0, HALF, "act")
+        for t in range(4):
+            sig(0, 0, t)
         for j in range(4, 8):
-            order_rows("ket", j, "dve" if j < 6 else "act")
-        sig_group(0, 0, 0, 0)
-        sig_group(0, 0, 0, 1)
-        sig_group(0, 0, 1, 0)
-        sig_group(0, 0, 1, 1)
+            turn("ket", j, "act")
+        quant_woven("rho", 0, 0)
+        weave("sig", 0, 0)
+        quant_turned("ket", 1, 0, 2 * HALF)
+        rho(1, 0, 0)
         for j in range(4, 8):
-            if j == 7:
-                weave_sig(0, 0)
-            turn_rows("ket", j, "act" if j < 7 else "dve")
-        rho_group(0, 1, 1)
-        quant_turned("ket", 1, 0, 0, HALF)
-        quant_turned("ket", 1, 1, 0, HALF)
-        weave_rho(1, 0)
-        rho_group(0, 1, 2)
-        for j in range(4, 8):
-            order_rows("bra", j, "act")
-        sig_group(1, 0, 0, 0)
-        sig_group(1, 0, 0, 1)
-        quant_woven("rho", 1, 0)
-        sig_group(1, 0, 1, 0)
-        sig_group(1, 0, 1, 1)
+            turn("bra", j, "act")
         quant_woven("sig", 0, 0)
-        weave_sig(1, 0)
-        for j in range(4, 8):
-            turn_rows("bra", j, "act")
-            if j == 5:
-                quant_turned("bra", 1, 0, 0, 256)
-                quant_turned("bra", 1, 1, 0, 256)
-                quant_woven("sig", 1, 0)
-            if j == 7:
-                quant_turned("bra", 1, 0, 256, HALF)
-                quant_turned("bra", 1, 1, 256, HALF)
-        rho_group(0, 1, 3)
-        rho_group(1, 1, 0)
-        for i in range(4):
-            sig_group(0, 1, i // 2, i % 2)
-        weave_rho(0, 1)
-        for i in range(4):
-            out_group(0, 0, i, "act")
-        weave_sig(0, 1)
-        for i in range(4):
-            sig_group(1, 1, i // 2, i % 2)
-            if i == 0:
-                quant_woven("sig", 0, 1)
-        weave_sig(1, 1)
+        quant_bra(1, 0)
+        quant_bra(1, 1)
+        rho(1, 0, 1)
+        weave("rho", 0, 1, 0, HALF, "act")
+        sig(1, 0, 0)
+        sig(1, 0, 1)
+        rho(1, 0, 2)
+        sig(1, 0, 2)
+        sig(1, 0, 3)
+        rho(1, 0, 3)
+        weave("sig", 1, 0)
+        weave("rho", 1, 0, 0, HALF, "act")
+        sig(0, 1, 0)
+        quant_woven("sig", 1, 0)
+        sig(0, 1, 1)
+        rho(1, 1, 0)
         quant_woven("rho", 0, 1)
+        sig(0, 1, 2)
+        sig(0, 1, 3)
+        quant_woven("rho", 1, 0)
+        rho(1, 1, 1)
+        weave("sig", 0, 1, 0, HALF, "act")
+        sig(1, 1, 0)
+        sig(1, 1, 1)
+        outg("act", 0, 0, 0)
+        sig(1, 1, 2)
+        outg("act", 0, 0, 1)
+        sig(1, 1, 3)
+        quant_woven("sig", 0, 1)
+        weave("sig", 1, 1)
+        outg("act", 0, 0, 2)
+        outg("act", 0, 0, 3)
+        rho(1, 1, 2)
         quant_woven("sig", 1, 1)
-        rho_group(1, 1, 1)
-        rho_group(1, 1, 2)
-        rho_group(1, 1, 3)
-        weave_rho(1, 1, 0, 128)
-        weave_rho(1, 1, 128, 256)
+        rho(1, 1, 3)
+        weave("rho", 1, 1, 0, 128)
+        weave("rho", 1, 1, 128, 256)
         quant_woven("rho", 1, 1, 0, 128)
-        weave_rho(1, 1, 256, HALF)
+        weave("rho", 1, 1, 256, HALF)
         quant_woven("rho", 1, 1, 128, 256)
         quant_woven("rho", 1, 1, 256, HALF)
         for i in range(4):
-            out_group(0, 1, i, "act")
+            outg("act", 0, 1, i)
         for i in range(4):
             for ch in range(2):
                 if i == 3 and ch == 1:
-                    out_half(1, 1, 3, 0, "act")
-                    out_half(1, 1, 3, 1, "dve")
+                    outg("act", 1, 1, 3, 0, 256)
+                    outg("dve", 1, 1, 3, 256, HALF)
                 else:
-                    out_group(1, ch, i, "dve" if ch == 0 else "act")
+                    outg("dve" if ch == 0 else "act", 1, ch, i)

@@ -44,7 +44,7 @@ def tile_two_copy_overlap_s12_kernel(
         tiny = kept("tiny", [P, 16], F32)
         filt_raw = kept("filt_raw", [P, 2, 16], BF16)
         filt_col = kept("filt_col", [P, 2, 4], F32)
-        rows = {(w, j): kept("%s_rows%d" % (w, j), [P, F], BF16) for w in ("ket", "bra") for j in range(8)}
+        rows = {(w, j): kept("%s_rows%d" % (w, j), [P, 2, F], BF16) for w in ("ket", "bra") for j in range(4)}
         turned = {(w, g): kept("%s_turned%d" % (w, g), [P, 2 * HALF * 4], BF16) for w in ("ket", "bra") for g in range(2)}
         codes = {(w, g): kept("%s_codes%d" % (w, g), [P, 2 * HALF], U32) for w in ("ket", "bra") for g in range(2)}
         scales = {(w, g): kept("%s_scales%d" % (w, g), [P, 2 * HALF], U8) for w in ("ket", "bra") for g in range(2)}
@@ -54,7 +54,7 @@ def tile_two_copy_overlap_s12_kernel(
         l_scale = [kept("l_scale%d" % g, [P, 4, 4, P], U8) for g in range(2)]
         r_words = [kept("r_words%d" % h, [P, 4, 2 * HALF], U8) for h in range(2)]
         r_scale = [kept("r_scale%d" % h, [P, 4, HALF], U8) for h in range(2)]
-        coh_sb = {(g, ch): kept("coh%d%d" % (g, ch), [P, 4, HALF], BF16) for g in range(2) for ch in range(2)}
+        coh_sb = [kept("coh%d" % g, [P, 4, A], BF16) for g in range(2)]
         q_codes = {(w, g, h): kept("%s_q%d%d" % (w, g, h), [P, HALF], U32) for w in ("rho", "sig") for g in range(2) for h in range(2)}
         q_scales = {(w, g, h): kept("%s_s%d%d" % (w, g, h), [P, HALF], U8) for w in ("rho", "sig") for g in range(2) for h in range(2)}
         flat = {}
@@ -62,7 +62,7 @@ def tile_two_copy_overlap_s12_kernel(
 
         def load_rows(w, j):
             src = ket if w == "ket" else bra
-            nc.sync.dma_start(out=rows[w, j][:], in_=src[j * P : (j + 1) * P, :])
+            nc.sync.dma_start(out=rows[w, j][:], in_=src[2 * j * P : 2 * (j + 1) * P, :].rearrange("(s p) f -> p s f", s=2))
 
         def load_scales(plane, src, h):
             by_row = src.bitcast(I32).rearrange("e (q r) n -> r q e n", r=4)
@@ -73,10 +73,10 @@ def tile_two_copy_overlap_s12_kernel(
             view = src.bitcast(I32).rearrange("e p n -> p e n")
             queue.dma_start(out=tile[:, e0:e1, :].bitcast(I32), in_=view[:, e0:e1, h * 256 : (h + 1) * 256])
 
-        def load_coh(g, ch):
+        def load_coh(g):
             view = coh.rearrange("(g p t j) c -> g j p t c", g=2, t=4, j=4)
             for j in range(4):
-                nc.sync.dma_start(out=coh_sb[g, ch][j:P:4, :, :], in_=view[g][j][:, :, ch * HALF : (ch + 1) * HALF])
+                nc.sync.dma_start(out=coh_sb[g][j:P:4, :, :], in_=view[g][j])
 
         def zero(engine, plane):
             engine.memset(plane[:].rearrange("p e n -> p (e n)").bitcast(I32), 0)
@@ -95,13 +95,13 @@ def tile_two_copy_overlap_s12_kernel(
             copy_on(
                 engine,
                 ordered[w, j][:].rearrange("k (h u p) -> k h u p", h=2, u=2),
-                rows[w, j][:].bitcast(F32).rearrange("k (h p u) -> k h u p", h=2, u=2),
+                rows[w, j // 2][:, j % 2, :].bitcast(F32).rearrange("k (h p u) -> k h u p", h=2, u=2),
             )
 
         def turn_mm(w, j):
             bank = next_bank()
             turned_bank[w, j] = bank
-            words = rows[w, j][:].bitcast(F32)
+            words = rows[w, j // 2][:, j % 2, :].bitcast(F32)
             for u in range(2):
                 for h in range(2):
                     if (w, j) in ordered:
@@ -125,8 +125,8 @@ def tile_two_copy_overlap_s12_kernel(
             else:
                 copy_on(
                     engine,
-                    dst.rearrange("p (h jj c u) -> p jj h c u", h=2, jj=4, u=2)[:, jj],
-                    bank[:].rearrange("p (u h c) -> p h c u", u=2, h=2),
+                    dst.rearrange("p (jj x u) -> p jj x u", jj=4, u=2)[:, jj],
+                    bank[:].rearrange("p (u x) -> p x u", u=2),
                 )
 
         def quant_turned(w, g, c0, c1):
@@ -188,27 +188,33 @@ def tile_two_copy_overlap_s12_kernel(
                 in_=woven[w, g, h][:, 4 * c0 : 4 * c1],
             )
 
-        def sig_mm(g, ch, t):
+        def sig_mm(g, ch, jj):
             bank = next_bank()
-            held["sig", g, ch, t] = bank
-            for h in range(2):
-                m_cols = slice(HALF * h + P * t, HALF * h + P * (t + 1))
-                cols = slice(HALF * h, HALF * (h + 1))
-                nc.tensor.matmul_mx(
-                    out=bank[:],
-                    lhsT=codes["ket", g][:, m_cols].bitcast(FP8X4),
-                    lhsT_scale=scales["ket", g][:, m_cols],
-                    rhs=codes["bra", ch][:, cols].bitcast(FP8X4),
-                    rhs_scale=scales["bra", ch][:, cols],
-                    start=(h == 0),
-                    stop=(h == 1),
-                )
+            held["sig", g, ch, jj] = bank
+            for t in range(4):
+                for h in range(2):
+                    m_cols = slice(HALF * h + P * t, HALF * h + P * (t + 1))
+                    cols = slice(256 * jj + P * h, 256 * jj + P * (h + 1))
+                    nc.tensor.matmul_mx(
+                        out=bank[:, P * t : P * (t + 1)],
+                        lhsT=codes["ket", g][:, m_cols].bitcast(FP8X4),
+                        lhsT_scale=scales["ket", g][:, m_cols],
+                        rhs=codes["bra", ch][:, cols].bitcast(FP8X4),
+                        rhs_scale=scales["bra", ch][:, cols],
+                        start=(h == 0),
+                        stop=(h == 1),
+                    )
 
-        def sig_out(g, ch, t):
-            bank = held["sig", g, ch, t]
-            if t == 0:
-                flat["sig", g, ch] = stage.tile([P, 4, HALF], BF16, name="sig_flat", bufs=2, align_bytes=64)
-            nc.vector.tensor_tensor(out=flat["sig", g, ch][:, t, :], in0=bank[:], in1=coh_sb[g, ch][:, t, :], op=MULT)
+        def sig_out(g, ch, jj):
+            if jj == 0:
+                woven["sig", g, ch] = stage.tile([P, HALF * 4], BF16, name="woven", bufs=4, align_bytes=64)
+            col0 = HALF * ch + P * jj
+            nc.vector.tensor_tensor(
+                out=woven["sig", g, ch][:, HALF * jj : HALF * (jj + 1)].rearrange("p (c i t) -> p c t i", i=4, t=4),
+                in0=held["sig", g, ch, jj][:].rearrange("p (t c i) -> p c t i", t=4, i=4),
+                in1=coh_sb[g][:, :, col0 : col0 + P].rearrange("p t (c i) -> p c t i", i=4),
+                op=MULT,
+            )
 
         def warm_up(count):
             blank = kept("blank", [P, HALF], BF16)
@@ -249,8 +255,7 @@ def tile_two_copy_overlap_s12_kernel(
             nc.sync.dma_start(out=out[row0 : row0 + P, HALF * ch + c0 : HALF * ch + c1], in_=result[:])
 
         def quant_bra(ch, x):
-            for h in range(2):
-                quant_turned("bra", ch, HALF * h + 256 * x, HALF * h + 256 * (x + 1))
+            quant_turned("bra", ch, HALF * x, HALF * (x + 1))
 
         def rho(g, ah, t):
             rho_mm(g, ah, t)
@@ -268,6 +273,30 @@ def tile_two_copy_overlap_s12_kernel(
             out_mm(ah, ch, i, c0, c1)
             out_store(engine, ah, ch, i, c0, c1)
 
+        def out_pair(engine, ah, ip, cq):
+            bank = next_bank()
+            cols = slice(256 * cq, 256 * (cq + 1))
+            for s in range(2):
+                a_cols = slice(P * (2 * ip + s), P * (2 * ip + s + 1))
+                for g in range(2):
+                    nc.tensor.matmul_mx(
+                        out=bank[:, 256 * s : 256 * (s + 1)],
+                        lhsT=q_codes["rho", g, ah][:, a_cols].bitcast(FP8X4),
+                        lhsT_scale=q_scales["rho", g, ah][:, a_cols],
+                        rhs=q_codes["sig", g, 1][:, cols].bitcast(FP8X4),
+                        rhs_scale=q_scales["sig", g, 1][:, cols],
+                        start=(g == 0),
+                        stop=(g == 1),
+                    )
+            result = stage.tile([P, HALF], F32, name="result", bufs=8, align_bytes=64)
+            copy_on(engine, result[:], bank[:])
+            row0 = HALF * ah + 2 * P * ip
+            col0 = HALF + 256 * cq
+            nc.sync.dma_start(
+                out=out[row0 : row0 + 2 * P, col0 : col0 + 256].rearrange("(s p) c -> p s c", s=2),
+                in_=result[:].rearrange("p (s c) -> p s c", s=2),
+            )
+
 
         load_words(l_raw[0], ref_bra_words, 0, 0, 2)
         load_words(r_words[0], ref_ket_words, 0, 0, 2)
@@ -277,7 +306,7 @@ def tile_two_copy_overlap_s12_kernel(
         make_identity(nc, ident[:])
         zero(nc.vector, l_scale_raw[0])
         zero(nc.vector, r_scale[0])
-        warm_up(18)
+        warm_up(22)
         nc.vector.memset(tiny[:], 0.0)
         nc.scalar.activation(out=tiny[:, 8:9], in_=tiny[:, 0:1], func=COPY, scale=tiny[:, 1:2])
         zero(nc.vector, r_scale[1])
@@ -289,20 +318,16 @@ def tile_two_copy_overlap_s12_kernel(
         load_words(r_words[0], ref_ket_words, 0, 2, 4)
         load_scales(r_scale[1], ref_ket_scales, 1)
         load_words(r_words[1], ref_ket_words, 1, 0, 4)
-        for j in range(4):
-            load_rows("ket", j)
-        for j in range(4):
-            load_rows("bra", j)
+        for w in ("ket", "bra"):
+            load_rows(w, 0)
+            load_rows(w, 1)
         load_scales(l_scale_raw[1], ref_bra_scales, 1)
         load_words(l_raw[1], ref_bra_words, 1, 0, 4)
-        load_coh(0, 0)
-        for j in range(4, 8):
-            load_rows("ket", j)
-        for j in range(4, 8):
-            load_rows("bra", j)
-        load_coh(1, 0)
-        load_coh(0, 1)
-        load_coh(1, 1)
+        load_coh(0)
+        for w in ("ket", "bra"):
+            load_rows(w, 2)
+            load_rows(w, 3)
+        load_coh(1)
 
         order_l_words(0, 0, 2)
         order_l_scales(0)
@@ -320,69 +345,62 @@ def tile_two_copy_overlap_s12_kernel(
             for e in range(2, 4):
                 rho_pass(held["rho", 0, 0, t], 0, 0, t, e)
             rho_out(0, 0, t)
-        for j in range(4):
-            order_rows("ket", j, "dve")
         rho(0, 1, 0)
         rho(0, 1, 1)
-        for j in range(4):
-            order_rows("bra", j, "dve")
+        for w in ("ket", "bra"):
+            for j in range(4):
+                order_rows(w, j, "dve")
+            if w == "ket":
+                weave("rho", 0, 0)
+        rho(0, 1, 2)
         for j in range(4):
             turn("ket", j, "dve" if j % 2 else "act")
+            if j == 1:
+                order_l_scales(1)
+        order_l_words(1, 0, 4)
         quant_turned("ket", 0, 0, 2 * HALF)
         for j in range(4):
             turn("bra", j, "act")
             if j % 2:
                 quant_bra(0, j // 2)
-        rho(0, 1, 2)
-        order_l_scales(1)
         rho(0, 1, 3)
-        order_l_words(1, 0, 4)
-        weave("rho", 0, 0, 0, HALF, "act")
-        for t in range(4):
-            sig(0, 0, t)
+        rho(1, 0, 0)
+        quant_woven("rho", 0, 0)
+        rho(1, 0, 1)
+        for j in range(4):
+            sig(0, 0, j)
+            order_rows("ket", 4 + j, "act")
         for j in range(4, 8):
             turn("ket", j, "act")
-        quant_woven("rho", 0, 0)
-        weave("sig", 0, 0)
+            order_rows("bra", j, "dve")
+        quant_woven("sig", 0, 0)
         quant_turned("ket", 1, 0, 2 * HALF)
-        rho(1, 0, 0)
+        rho(1, 0, 2)
         for j in range(4, 8):
             turn("bra", j, "act")
-        quant_woven("sig", 0, 0)
+        rho(1, 0, 3)
         quant_bra(1, 0)
         quant_bra(1, 1)
-        rho(1, 0, 1)
-        weave("rho", 0, 1, 0, HALF, "act")
-        sig(1, 0, 0)
-        sig(1, 0, 1)
-        rho(1, 0, 2)
-        sig(1, 0, 2)
-        sig(1, 0, 3)
-        rho(1, 0, 3)
-        weave("sig", 1, 0)
+        for j in range(4):
+            sig(1, 0, j)
         weave("rho", 1, 0, 0, HALF, "act")
-        sig(0, 1, 0)
         quant_woven("sig", 1, 0)
-        sig(0, 1, 1)
         rho(1, 1, 0)
-        quant_woven("rho", 0, 1)
-        sig(0, 1, 2)
-        sig(0, 1, 3)
+        sig(0, 1, 0)
+        sig(0, 1, 1)
         quant_woven("rho", 1, 0)
         rho(1, 1, 1)
-        weave("sig", 0, 1, 0, HALF, "act")
-        sig(1, 1, 0)
-        sig(1, 1, 1)
-        outg("act", 0, 0, 0)
-        sig(1, 1, 2)
-        outg("act", 0, 0, 1)
-        sig(1, 1, 3)
-        quant_woven("sig", 0, 1)
-        weave("sig", 1, 1)
-        outg("act", 0, 0, 2)
-        outg("act", 0, 0, 3)
-        rho(1, 1, 2)
+        weave("rho", 0, 1, 0, HALF, "act")
+        sig(0, 1, 2)
+        sig(0, 1, 3)
+        for j in range(4):
+            outg("act", 0, 0, j)
+            sig(1, 1, j)
+            if j == 0:
+                quant_woven("sig", 0, 1)
+        quant_woven("rho", 0, 1)
         quant_woven("sig", 1, 1)
+        rho(1, 1, 2)
         rho(1, 1, 3)
         weave("rho", 1, 1, 0, 128)
         weave("rho", 1, 1, 128, 256)

@@ -64,9 +64,9 @@ def tile_two_copy_overlap_s12_kernel(
             src = ket if w == "ket" else bra
             nc.sync.dma_start(out=rows[w, j][:], in_=src[2 * j * P : 2 * (j + 1) * P, :].rearrange("(s p) f -> p s f", s=2))
 
-        def load_scales(plane, src, h):
+        def load_scales(plane, src, h, r0=0, r1=4):
             by_row = src.bitcast(I32).rearrange("e (q r) n -> r q e n", r=4)
-            for r in range(4):
+            for r in range(r0, r1):
                 nc.sync.dma_start(out=plane[r:P:32, :, :].bitcast(I32), in_=by_row[r][:, :, h * P : (h + 1) * P])
 
         def load_words(tile, src, h, e0, e1, queue=nc.sync):
@@ -77,6 +77,10 @@ def tile_two_copy_overlap_s12_kernel(
             view = coh.rearrange("(g p t j) c -> g j p t c", g=2, t=4, j=4)
             for j in range(4):
                 nc.sync.dma_start(out=coh_sb[g][j:P:4, :, :], in_=view[g][j])
+
+        def load_filt(j):
+            by_16 = filt.rearrange("(g p s) -> p g s", g=2, s=16)
+            nc.sync.dma_start(out=filt_raw[j:P:4, :, 0:13], in_=by_16[:, :, j : j + 13])
 
         def zero(engine, plane):
             engine.memset(plane[:].rearrange("p e n -> p (e n)").bitcast(I32), 0)
@@ -166,11 +170,11 @@ def tile_two_copy_overlap_s12_kernel(
             for e in range(4):
                 rho_pass(held["rho", g, ah, t], g, ah, t, e)
 
-        def rho_out(g, ah, t):
+        def rho_out(g, ah, t, c0=0, c1=HALF):
             bank = held["rho", g, ah, t]
             if t == 0:
                 flat["rho", g, ah] = stage.tile([P, 4, HALF], BF16, name="rho_flat", bufs=3, align_bytes=64)
-            nc.scalar.activation(out=flat["rho", g, ah][:, t, :], in_=bank[:], func=COPY, scale=filt_col[:, g, t : t + 1])
+            nc.scalar.activation(out=flat["rho", g, ah][:, t, c0:c1], in_=bank[:, c0:c1], func=COPY, scale=filt_col[:, g, t : t + 1])
 
         def weave(w, g, ah, c0=0, c1=HALF, engine="dve"):
             if c0 == 0:
@@ -273,37 +277,16 @@ def tile_two_copy_overlap_s12_kernel(
             out_mm(ah, ch, i, c0, c1)
             out_store(engine, ah, ch, i, c0, c1)
 
-        def out_pair(engine, ah, ip, cq):
-            bank = next_bank()
-            cols = slice(256 * cq, 256 * (cq + 1))
-            for s in range(2):
-                a_cols = slice(P * (2 * ip + s), P * (2 * ip + s + 1))
-                for g in range(2):
-                    nc.tensor.matmul_mx(
-                        out=bank[:, 256 * s : 256 * (s + 1)],
-                        lhsT=q_codes["rho", g, ah][:, a_cols].bitcast(FP8X4),
-                        lhsT_scale=q_scales["rho", g, ah][:, a_cols],
-                        rhs=q_codes["sig", g, 1][:, cols].bitcast(FP8X4),
-                        rhs_scale=q_scales["sig", g, 1][:, cols],
-                        start=(g == 0),
-                        stop=(g == 1),
-                    )
-            result = stage.tile([P, HALF], F32, name="result", bufs=8, align_bytes=64)
-            copy_on(engine, result[:], bank[:])
-            row0 = HALF * ah + 2 * P * ip
-            col0 = HALF + 256 * cq
-            nc.sync.dma_start(
-                out=out[row0 : row0 + 2 * P, col0 : col0 + 256].rearrange("(s p) c -> p s c", s=2),
-                in_=result[:].rearrange("p (s c) -> p s c", s=2),
-            )
+        def out_both(i):
+            wide = stage.tile([P, A], F32, name="wide", bufs=3, align_bytes=64)
+            for ch in range(2):
+                out_mm(1, ch, i)
+                copy_on("act" if ch == 0 else "dve", wide[:, HALF * ch : HALF * (ch + 1)], held["out", 1, ch, i, 0][:])
+            nc.sync.dma_start(out=out[HALF + P * i : HALF + P * (i + 1), :], in_=wide[:])
 
 
         load_words(l_raw[0], ref_bra_words, 0, 0, 2)
         load_words(r_words[0], ref_ket_words, 0, 0, 2)
-        by_16 = filt.rearrange("(g p s) -> p g s", g=2, s=16)
-        for j in range(4):
-            nc.gpsimd.dma_start(out=filt_raw[j:P:4, :, 0:13], in_=by_16[:, :, j : j + 13])
-        make_identity(nc, ident[:])
         zero(nc.vector, l_scale_raw[0])
         zero(nc.vector, r_scale[0])
         warm_up(22)
@@ -318,6 +301,9 @@ def tile_two_copy_overlap_s12_kernel(
         load_words(r_words[0], ref_ket_words, 0, 2, 4)
         load_scales(r_scale[1], ref_ket_scales, 1)
         load_words(r_words[1], ref_ket_words, 1, 0, 4)
+        by_16 = filt.rearrange("(g p s) -> p g s", g=2, s=16)
+        for j in range(4):
+            nc.sync.dma_start(out=filt_raw[j:P:4, :, 0:13], in_=by_16[:, :, j : j + 13])
         for w in ("ket", "bra"):
             load_rows(w, 0)
             load_rows(w, 1)
@@ -331,6 +317,8 @@ def tile_two_copy_overlap_s12_kernel(
 
         order_l_words(0, 0, 2)
         order_l_scales(0)
+        nc.vector.memset(ident[:], 0.0)
+        make_identity(nc, ident[:], nomemset=True)
         order_l_words(0, 2, 4)
         nc.vector.tensor_copy(
             out=perm[:].rearrange("k (t p j) -> k t p j", t=4, j=4), in_=ident[:].rearrange("k (p t j) -> k t p j", t=4, j=4)
@@ -354,9 +342,8 @@ def tile_two_copy_overlap_s12_kernel(
                 weave("rho", 0, 0)
         rho(0, 1, 2)
         for j in range(4):
-            turn("ket", j, "dve" if j % 2 else "act")
-            if j == 1:
-                order_l_scales(1)
+            turn("ket", j, "act")
+        order_l_scales(1)
         order_l_words(1, 0, 4)
         quant_turned("ket", 0, 0, 2 * HALF)
         for j in range(4):
@@ -367,14 +354,15 @@ def tile_two_copy_overlap_s12_kernel(
         rho(1, 0, 0)
         quant_woven("rho", 0, 0)
         rho(1, 0, 1)
+        for j in range(4, 8):
+            order_rows("ket", j, "dve" if j < 6 else "act")
         for j in range(4):
             sig(0, 0, j)
-            order_rows("ket", 4 + j, "act")
         for j in range(4, 8):
             turn("ket", j, "act")
             order_rows("bra", j, "dve")
-        quant_woven("sig", 0, 0)
         quant_turned("ket", 1, 0, 2 * HALF)
+        quant_woven("sig", 0, 0)
         rho(1, 0, 2)
         for j in range(4, 8):
             turn("bra", j, "act")
@@ -394,12 +382,12 @@ def tile_two_copy_overlap_s12_kernel(
         sig(0, 1, 2)
         sig(0, 1, 3)
         for j in range(4):
-            outg("act", 0, 0, j)
             sig(1, 1, j)
+            outg("act", 0, 0, j)
             if j == 0:
                 quant_woven("sig", 0, 1)
-        quant_woven("rho", 0, 1)
         quant_woven("sig", 1, 1)
+        quant_woven("rho", 0, 1)
         rho(1, 1, 2)
         rho(1, 1, 3)
         weave("rho", 1, 1, 0, 128)

@@ -41,7 +41,6 @@ def tile_two_copy_overlap_s12_kernel(
 
         ident = kept("ident", [P, P], F32)
         perm = kept("perm", [P, P], F32)
-        tiny = kept("tiny", [P, 16], F32)
         filt_raw = kept("filt_raw", [P, 2, 16], BF16)
         filt_col = kept("filt_col", [P, 2, 4], F32)
         rows = {(w, j): kept("%s_rows%d" % (w, j), [P, 2, F], BF16) for w in ("ket", "bra") for j in range(4)}
@@ -220,23 +219,6 @@ def tile_two_copy_overlap_s12_kernel(
                 op=MULT,
             )
 
-        def warm_up(count):
-            blank = kept("blank", [P, HALF], BF16)
-            blank_codes = kept("blank_codes", [P, P], U32)
-            blank_scales = kept("blank_scales", [P, P], U8)
-            nc.vector.memset(blank[:], 0.0)
-            nc.vector.quantize_mx(out=blank_codes[:].bitcast(FP8X4), scales=blank_scales[:], in_=blank[:])
-            for i in range(count):
-                nc.tensor.matmul_mx(
-                    out=banks[7][:, P * (i % 4) : P * (i % 4 + 1)],
-                    lhsT=blank_codes[:].bitcast(FP8X4),
-                    lhsT_scale=blank_scales[:],
-                    rhs=blank_codes[:].bitcast(FP8X4),
-                    rhs_scale=blank_scales[:],
-                    start=True,
-                    stop=True,
-                )
-
         def out_mm(ah, ch, i, c0=0, c1=HALF):
             bank = next_bank()
             held["out", ah, ch, i, c0] = bank
@@ -289,9 +271,6 @@ def tile_two_copy_overlap_s12_kernel(
         load_words(r_words[0], ref_ket_words, 0, 0, 2)
         zero(nc.vector, l_scale_raw[0])
         zero(nc.vector, r_scale[0])
-        warm_up(22)
-        nc.vector.memset(tiny[:], 0.0)
-        nc.scalar.activation(out=tiny[:, 8:9], in_=tiny[:, 0:1], func=COPY, scale=tiny[:, 1:2])
         zero(nc.vector, r_scale[1])
         zero(nc.vector, l_scale_raw[1])
 

@@ -145,6 +145,14 @@ def tile_two_copy_overlap_s12_kernel(
                 in_=l_scale_raw[g][:].rearrange("k e n -> k (e n)").bitcast(I32).rearrange("k (x t) -> k t x", t=4),
             )
 
+        def order_l_scale_rows(g, e0, e1):
+            for q in range(4):
+                live = slice(32 * q, 32 * q + 4)
+                nc.vector.tensor_copy(
+                    out=l_scale[g][live, :, e0:e1, :].rearrange("k t e n -> k t (e n)").bitcast(I32),
+                    in_=l_scale_raw[g][live, e0:e1, :].rearrange("k e n -> k (e n)").bitcast(I32).rearrange("k (x t) -> k t x", t=4),
+                )
+
         def order_l_words(g, e0, e1):
             nc.vector.tensor_copy(
                 out=l_words[g][:, :, e0:e1, :].rearrange("k t e n -> k t (e n)").bitcast(I32).rearrange("k t (x w) -> k t x w", w=2),
@@ -259,50 +267,53 @@ def tile_two_copy_overlap_s12_kernel(
             out_mm(ah, ch, i, c0, c1)
             out_store(engine, ah, ch, i, c0, c1)
 
-        def out_both(i):
-            wide = stage.tile([P, A], F32, name="wide", bufs=3, align_bytes=64)
-            for ch in range(2):
-                out_mm(1, ch, i)
-                copy_on("act" if ch == 0 else "dve", wide[:, HALF * ch : HALF * (ch + 1)], held["out", 1, ch, i, 0][:])
-            nc.sync.dma_start(out=out[HALF + P * i : HALF + P * (i + 1), :], in_=wide[:])
-
-
+        load_scales(l_scale_raw[0], ref_bra_scales, 0)
         load_words(l_raw[0], ref_bra_words, 0, 0, 2)
         load_words(r_words[0], ref_ket_words, 0, 0, 2)
-        zero(nc.vector, l_scale_raw[0])
         zero(nc.vector, r_scale[0])
+        nc.vector.memset(l_scale[0][:].rearrange("p t e n -> p (t e n)").bitcast(I32), 0)
+        nc.vector.memset(ident[:], 0.0)
+        make_identity(nc, ident[:], nomemset=True)
         zero(nc.vector, r_scale[1])
         zero(nc.vector, l_scale_raw[1])
 
-        load_scales(l_scale_raw[0], ref_bra_scales, 0)
         load_scales(r_scale[0], ref_ket_scales, 0)
         load_words(l_raw[0], ref_bra_words, 0, 2, 4)
         load_words(r_words[0], ref_ket_words, 0, 2, 4)
         load_scales(r_scale[1], ref_ket_scales, 1)
         load_words(r_words[1], ref_ket_words, 1, 0, 4)
-        by_16 = filt.rearrange("(g p s) -> p g s", g=2, s=16)
         for j in range(4):
-            nc.sync.dma_start(out=filt_raw[j:P:4, :, 0:13], in_=by_16[:, :, j : j + 13])
-        for w in ("ket", "bra"):
-            load_rows(w, 0)
-            load_rows(w, 1)
+            load_filt(j)
+        load_rows("ket", 0)
+        load_rows("ket", 1)
         load_scales(l_scale_raw[1], ref_bra_scales, 1)
         load_words(l_raw[1], ref_bra_words, 1, 0, 4)
+        load_rows("ket", 2)
+        load_rows("ket", 3)
+        for j in range(4):
+            load_rows("bra", j)
         load_coh(0)
-        for w in ("ket", "bra"):
-            load_rows(w, 2)
-            load_rows(w, 3)
         load_coh(1)
 
+        order_l_scale_rows(0, 0, 2)
         order_l_words(0, 0, 2)
-        order_l_scales(0)
-        nc.vector.memset(ident[:], 0.0)
-        make_identity(nc, ident[:], nomemset=True)
+        order_l_scale_rows(0, 2, 4)
         order_l_words(0, 2, 4)
-        nc.vector.tensor_copy(
-            out=perm[:].rearrange("k (t p j) -> k t p j", t=4, j=4), in_=ident[:].rearrange("k (p t j) -> k t p j", t=4, j=4)
+        nc.scalar.activation(
+            out=perm[:].rearrange("k (t p j) -> k t p j", t=4, j=4),
+            in_=ident[:].rearrange("k (p t j) -> k t p j", t=4, j=4),
+            func=COPY,
         )
         nc.scalar.copy(out=filt_col[:], in_=filt_raw[:, :, 0:13:4])
+
+        def turn_run(w, half, engines):
+            for j in range(4):
+                turn(w, 4 * half + j, engines[j])
+
+        def order_run(w, half):
+            for j in range(4):
+                order_rows(w, 4 * half + j, "dve")
+
         for t in range(4):
             held["rho", 0, 0, t] = next_bank()
         for e in range(2):
@@ -313,74 +324,74 @@ def tile_two_copy_overlap_s12_kernel(
                 rho_pass(held["rho", 0, 0, t], 0, 0, t, e)
             rho_out(0, 0, t)
         rho(0, 1, 0)
+        weave("rho", 0, 0)
         rho(0, 1, 1)
-        for w in ("ket", "bra"):
-            for j in range(4):
-                order_rows(w, j, "dve")
-            if w == "ket":
-                weave("rho", 0, 0)
+        order_run("ket", 0)
+        quant_woven("rho", 0, 0)
         rho(0, 1, 2)
-        for j in range(4):
-            turn("ket", j, "act")
+        rho(0, 1, 3)
         order_l_scales(1)
         order_l_words(1, 0, 4)
-        quant_turned("ket", 0, 0, 2 * HALF)
-        for j in range(4):
-            turn("bra", j, "act")
-            if j % 2:
-                quant_bra(0, j // 2)
-        rho(0, 1, 3)
+        turn_run("ket", 0, ("act", "dve", "act", "act"))
+        weave("rho", 0, 1)
+        order_run("ket", 1)
         rho(1, 0, 0)
-        quant_woven("rho", 0, 0)
         rho(1, 0, 1)
-        for j in range(4, 8):
-            order_rows("ket", j, "dve" if j < 6 else "act")
-        for j in range(4):
-            sig(0, 0, j)
-        for j in range(4, 8):
-            turn("ket", j, "act")
-            order_rows("bra", j, "dve")
-        quant_turned("ket", 1, 0, 2 * HALF)
-        quant_woven("sig", 0, 0)
+        quant_turned("ket", 0, 0, HALF)
+        quant_turned("ket", 0, HALF, 2 * HALF)
+        turn_run("ket", 1, ("act", "dve", "act", "act"))
+        quant_woven("rho", 0, 1)
+        order_run("bra", 0)
         rho(1, 0, 2)
-        for j in range(4, 8):
-            turn("bra", j, "act")
         rho(1, 0, 3)
-        quant_bra(1, 0)
-        quant_bra(1, 1)
-        for j in range(4):
-            sig(1, 0, j)
-        weave("rho", 1, 0, 0, HALF, "act")
-        quant_woven("sig", 1, 0)
+        quant_turned("ket", 1, 0, HALF)
+        quant_turned("ket", 1, HALF, 2 * HALF)
+        turn_run("bra", 0, ("act", "dve", "act", "dve"))
+        quant_bra(0, 0)
+        order_run("bra", 1)
+        quant_bra(0, 1)
         rho(1, 1, 0)
-        sig(0, 1, 0)
-        sig(0, 1, 1)
-        quant_woven("rho", 1, 0)
+        weave("rho", 1, 0, 0, HALF, "act")
         rho(1, 1, 1)
-        weave("rho", 0, 1, 0, HALF, "act")
+        sig(0, 0, 0)
+        sig(0, 0, 1)
+        turn_run("bra", 1, ("act", "act", "act", "act"))
+        quant_woven("rho", 1, 0)
+        sig(0, 0, 2)
+        sig(0, 0, 3)
+        rho(1, 1, 2)
+        sig(1, 0, 0)
+        quant_woven("sig", 0, 0)
+        sig(1, 0, 1)
+        quant_bra(1, 0)
+        rho(1, 1, 3)
+        weave("rho", 1, 1, 0, HALF, "act")
+        sig(1, 0, 2)
+        quant_bra(1, 1)
+        sig(1, 0, 3)
+        sig(0, 1, 0)
+        quant_woven("sig", 1, 0)
+        sig(0, 1, 1)
         sig(0, 1, 2)
         sig(0, 1, 3)
-        for j in range(4):
-            sig(1, 1, j)
-            outg("act", 0, 0, j)
-            if j == 0:
-                quant_woven("sig", 0, 1)
-        quant_woven("sig", 1, 1)
-        quant_woven("rho", 0, 1)
-        rho(1, 1, 2)
-        rho(1, 1, 3)
-        weave("rho", 1, 1, 0, 128)
-        weave("rho", 1, 1, 128, 256)
-        quant_woven("rho", 1, 1, 0, 128)
-        weave("rho", 1, 1, 256, HALF)
-        quant_woven("rho", 1, 1, 128, 256)
-        quant_woven("rho", 1, 1, 256, HALF)
+        quant_woven("rho", 1, 1)
+        outg("act", 0, 0, 0)
+        sig(1, 1, 0)
+        outg("act", 0, 0, 1)
+        quant_woven("sig", 0, 1)
+        sig(1, 1, 1)
+        outg("act", 0, 0, 2)
+        sig(1, 1, 2)
+        quant_woven("sig", 1, 1, 0, 256)
+        outg("act", 0, 0, 3)
+        sig(1, 1, 3)
+        quant_woven("sig", 1, 1, 256, HALF)
         for i in range(4):
-            outg("act", 0, 1, i)
-        for i in range(4):
-            for ch in range(2):
-                if i == 3 and ch == 1:
+            outg("act", 1, 0, i)
+        for ah in range(2):
+            for i in range(4):
+                if ah == 1 and i == 3:
                     outg("act", 1, 1, 3, 0, 256)
                     outg("dve", 1, 1, 3, 256, HALF)
                 else:
-                    outg("dve" if ch == 0 else "act", 1, ch, i)
+                    outg("dve" if i % 2 == 0 else "act", ah, 1, i)

@@ -94,23 +94,20 @@ def tile_two_copy_overlap_s12_kernel(
                 nc.vector.tensor_copy(out=out, in_=in_)
 
         def order_rows(w, j, engine):
-            ordered[w, j] = stage.tile([P, HALF], F32, name="ordered", bufs=8, align_bytes=64)
+            ordered[w, j] = stage.tile([P, 2 * HALF], F32, name="ordered", bufs=4, align_bytes=64)
             copy_on(
                 engine,
-                ordered[w, j][:].rearrange("k (h u p) -> k h u p", h=2, u=2),
-                rows[w, j // 2][:, j % 2, :].bitcast(F32).rearrange("k (h p u) -> k h u p", h=2, u=2),
+                ordered[w, j][:].rearrange("k (x u q i) -> k x u q i", x=4, u=2, i=8),
+                rows[w, j][:].rearrange("k s f -> k (s f)").bitcast(F32).rearrange("k (x q u i) -> k x u q i", x=4, u=2, i=8),
             )
 
         def turn_mm(w, j):
             bank = next_bank()
             turned_bank[w, j] = bank
-            words = rows[w, j // 2][:, j % 2, :].bitcast(F32)
             for u in range(2):
                 for h in range(2):
-                    if (w, j) in ordered:
-                        src = ordered[w, j][:, 256 * h + P * u : 256 * h + P * (u + 1)]
-                    else:
-                        src = words[:, 256 * h + u : 256 * (h + 1) : 2]
+                    w0 = HALF * (j % 2) + 256 * h + P * u
+                    src = ordered[w, j // 2][:, w0 : w0 + P]
                     nc.tensor.transpose(
                         bank[:, 256 * u + P * h : 256 * u + P * (h + 1)], src, (perm if w == "ket" else ident)[:]
                     )
@@ -128,8 +125,8 @@ def tile_two_copy_overlap_s12_kernel(
             else:
                 copy_on(
                     engine,
-                    dst.rearrange("p (jj x u) -> p jj x u", jj=4, u=2)[:, jj],
-                    bank[:].rearrange("p (u x) -> p x u", u=2),
+                    dst.rearrange("p (jp h j2 c u) -> p jp j2 h c u", jp=2, h=2, j2=2, u=2)[:, jj // 2, jj % 2],
+                    bank[:].rearrange("p (u h c) -> p h c u", u=2, h=2),
                 )
 
         def quant_turned(w, g, c0, c1):
@@ -199,15 +196,19 @@ def tile_two_copy_overlap_s12_kernel(
                 in_=woven[w, g, h][:, 4 * c0 : 4 * c1],
             )
 
+        paired = {}
+
         def sig_mm(g, ch, jj):
             bank = next_bank()
             held["sig", g, ch, jj] = bank
-            for t in range(4):
+            cq, tp = jj // 2, jj % 2
+            for t2 in range(2):
                 for h in range(2):
-                    m_cols = slice(HALF * h + P * t, HALF * h + P * (t + 1))
-                    cols = slice(256 * jj + P * h, 256 * jj + P * (h + 1))
+                    m0 = HALF * h + P * (2 * tp + t2)
+                    m_cols = slice(m0, m0 + P)
+                    cols = slice(HALF * cq + 256 * h, HALF * cq + 256 * (h + 1))
                     nc.tensor.matmul_mx(
-                        out=bank[:, P * t : P * (t + 1)],
+                        out=bank[:, 256 * t2 : 256 * (t2 + 1)],
                         lhsT=codes["ket", g][:, m_cols].bitcast(FP8X4),
                         lhsT_scale=scales["ket", g][:, m_cols],
                         rhs=codes["bra", ch][:, cols].bitcast(FP8X4),
@@ -217,14 +218,24 @@ def tile_two_copy_overlap_s12_kernel(
                     )
 
         def sig_out(g, ch, jj):
+            cq, tp = jj // 2, jj % 2
             if jj == 0:
-                woven["sig", g, ch] = stage.tile([P, HALF * 4], BF16, name="woven", bufs=4, align_bytes=64)
-            col0 = HALF * ch + P * jj
+                paired[g, ch] = stage.tile([P, 2, HALF, 2], BF16, name="paired", bufs=2, align_bytes=64)
+            col0 = HALF * ch + 256 * cq
             nc.vector.tensor_tensor(
-                out=woven["sig", g, ch][:, HALF * jj : HALF * (jj + 1)].rearrange("p (c i t) -> p c t i", i=4, t=4),
-                in0=held["sig", g, ch, jj][:].rearrange("p (t c i) -> p c t i", t=4, i=4),
-                in1=coh_sb[g][:, :, col0 : col0 + P].rearrange("p t (c i) -> p c t i", i=4),
+                out=paired[g, ch][:, tp, 256 * cq : 256 * (cq + 1), :],
+                in0=held["sig", g, ch, jj][:].rearrange("p (t c) -> p c t", t=2),
+                in1=coh_sb[g][:, 2 * tp : 2 * tp + 2, col0 : col0 + 256].rearrange("p t c -> p c t"),
                 op=MULT,
+            )
+
+        def weave_sig(g, ch, c0=0, c1=HALF, engine="dve"):
+            if c0 == 0:
+                woven["sig", g, ch] = stage.tile([P, HALF * 4], BF16, name="woven", bufs=4, align_bytes=64)
+            copy_on(
+                engine,
+                woven["sig", g, ch][:, 4 * c0 : 4 * c1].bitcast(F32).rearrange("p (c tp) -> p c tp", tp=2),
+                paired[g, ch][:].rearrange("p tp c t -> p tp (c t)").bitcast(F32)[:, :, c0:c1].rearrange("p tp c -> p c tp"),
             )
 
         def out_mm(ah, ch, i, c0=0, c1=HALF):
@@ -280,19 +291,21 @@ def tile_two_copy_overlap_s12_kernel(
         load_scales(r_scale[0], ref_ket_scales, 0)
         load_words(l_raw[0], ref_bra_words, 0, 2, 4)
         load_words(r_words[0], ref_ket_words, 0, 2, 4)
-        load_scales(r_scale[1], ref_ket_scales, 1)
-        load_words(r_words[1], ref_ket_words, 1, 0, 4)
         for j in range(4):
             load_filt(j)
         load_rows("ket", 0)
         load_rows("ket", 1)
-        load_scales(l_scale_raw[1], ref_bra_scales, 1)
-        load_words(l_raw[1], ref_bra_words, 1, 0, 4)
+        load_scales(r_scale[1], ref_ket_scales, 1)
+        load_words(r_words[1], ref_ket_words, 1, 0, 4)
         load_rows("ket", 2)
         load_rows("ket", 3)
-        for j in range(4):
-            load_rows("bra", j)
+        load_scales(l_scale_raw[1], ref_bra_scales, 1)
+        load_words(l_raw[1], ref_bra_words, 1, 0, 4)
+        load_rows("bra", 0)
+        load_rows("bra", 1)
         load_coh(0)
+        load_rows("bra", 2)
+        load_rows("bra", 3)
         load_coh(1)
 
         order_l_scale_rows(0, 0, 2)
@@ -310,10 +323,6 @@ def tile_two_copy_overlap_s12_kernel(
             for j in range(4):
                 turn(w, 4 * half + j, engines[j])
 
-        def order_run(w, half):
-            for j in range(4):
-                order_rows(w, 4 * half + j, "dve")
-
         for t in range(4):
             held["rho", 0, 0, t] = next_bank()
         for e in range(2):
@@ -323,68 +332,78 @@ def tile_two_copy_overlap_s12_kernel(
             for e in range(2, 4):
                 rho_pass(held["rho", 0, 0, t], 0, 0, t, e)
             rho_out(0, 0, t)
-        rho(0, 1, 0)
+        order_rows("ket", 0, "dve")
+        order_rows("ket", 1, "dve")
+        turn_run("ket", 0, ("dve", "dve", "act", "act"))
         weave("rho", 0, 0)
+        rho(0, 1, 0)
+        order_rows("ket", 2, "act")
         rho(0, 1, 1)
-        order_run("ket", 0)
+        order_rows("ket", 3, "dve")
         quant_woven("rho", 0, 0)
+        quant_turned("ket", 0, 0, 2 * HALF)
         rho(0, 1, 2)
         rho(0, 1, 3)
         order_l_scales(1)
         order_l_words(1, 0, 4)
-        turn_run("ket", 0, ("act", "dve", "act", "act"))
+        turn_run("ket", 1, ("act", "act", "act", "act"))
+        order_rows("bra", 0, "dve")
         weave("rho", 0, 1)
-        order_run("ket", 1)
+        order_rows("bra", 1, "dve")
         rho(1, 0, 0)
         rho(1, 0, 1)
-        quant_turned("ket", 0, 0, HALF)
-        quant_turned("ket", 0, HALF, 2 * HALF)
-        turn_run("ket", 1, ("act", "dve", "act", "act"))
         quant_woven("rho", 0, 1)
-        order_run("bra", 0)
+        quant_turned("ket", 1, 0, 2 * HALF)
+        turn_run("bra", 0, ("act", "act", "act", "act"))
+        order_rows("bra", 2, "dve")
         rho(1, 0, 2)
-        rho(1, 0, 3)
-        quant_turned("ket", 1, 0, HALF)
-        quant_turned("ket", 1, HALF, 2 * HALF)
-        turn_run("bra", 0, ("act", "dve", "act", "dve"))
         quant_bra(0, 0)
-        order_run("bra", 1)
+        order_rows("bra", 3, "dve")
+        rho(1, 0, 3)
         quant_bra(0, 1)
         rho(1, 1, 0)
-        weave("rho", 1, 0, 0, HALF, "act")
-        rho(1, 1, 1)
+        weave("rho", 1, 0)
         sig(0, 0, 0)
         sig(0, 0, 1)
         turn_run("bra", 1, ("act", "act", "act", "act"))
         quant_woven("rho", 1, 0)
         sig(0, 0, 2)
         sig(0, 0, 3)
-        rho(1, 1, 2)
-        sig(1, 0, 0)
-        quant_woven("sig", 0, 0)
-        sig(1, 0, 1)
+        rho(1, 1, 1)
         quant_bra(1, 0)
-        rho(1, 1, 3)
-        weave("rho", 1, 1, 0, HALF, "act")
-        sig(1, 0, 2)
+        weave_sig(0, 0, 0, HALF, "act")
+        sig(1, 0, 0)
+        sig(1, 0, 1)
         quant_bra(1, 1)
+        rho(1, 1, 2)
+        weave_sig(1, 0, 0, 256, "act")
+        quant_woven("sig", 0, 0)
+        sig(1, 0, 2)
         sig(1, 0, 3)
-        sig(0, 1, 0)
-        quant_woven("sig", 1, 0)
+        rho(1, 1, 3)
+        quant_woven("sig", 1, 0, 0, 256)
+        weave_sig(1, 0, 256, HALF)
+        sig_mm(0, 1, 0)
+        quant_woven("sig", 1, 0, 256, HALF)
+        sig_out(0, 1, 0)
+        weave("rho", 1, 1, 0, HALF, "act")
         sig(0, 1, 1)
         sig(0, 1, 2)
-        sig(0, 1, 3)
-        quant_woven("rho", 1, 1)
         outg("act", 0, 0, 0)
-        sig(1, 1, 0)
+        sig(0, 1, 3)
         outg("act", 0, 0, 1)
-        quant_woven("sig", 0, 1)
-        sig(1, 1, 1)
+        sig(1, 1, 0)
+        quant_woven("rho", 1, 1)
+        weave_sig(0, 1, 0, HALF, "act")
         outg("act", 0, 0, 2)
+        sig(1, 1, 1)
+        weave_sig(1, 1, 0, 256, "act")
         sig(1, 1, 2)
-        quant_woven("sig", 1, 1, 0, 256)
         outg("act", 0, 0, 3)
         sig(1, 1, 3)
+        quant_woven("sig", 0, 1)
+        weave_sig(1, 1, 256, HALF)
+        quant_woven("sig", 1, 1, 0, 256)
         quant_woven("sig", 1, 1, 256, HALF)
         for i in range(4):
             outg("act", 1, 0, i)

@@ -142,14 +142,6 @@ def tile_two_copy_overlap_s12_kernel(
                 in_=l_scale_raw[g][:].rearrange("k e n -> k (e n)").bitcast(I32).rearrange("k (x t) -> k t x", t=4),
             )
 
-        def order_l_scale_rows(g, e0, e1):
-            for q in range(4):
-                live = slice(32 * q, 32 * q + 4)
-                nc.vector.tensor_copy(
-                    out=l_scale[g][live, :, e0:e1, :].rearrange("k t e n -> k t (e n)").bitcast(I32),
-                    in_=l_scale_raw[g][live, e0:e1, :].rearrange("k e n -> k (e n)").bitcast(I32).rearrange("k (x t) -> k t x", t=4),
-                )
-
         def order_l_words(g, e0, e1):
             nc.vector.tensor_copy(
                 out=l_words[g][:, :, e0:e1, :].rearrange("k t e n -> k t (e n)").bitcast(I32).rearrange("k t (x w) -> k t x w", w=2),
@@ -278,16 +270,14 @@ def tile_two_copy_overlap_s12_kernel(
             out_mm(ah, ch, i, c0, c1)
             out_store(engine, ah, ch, i, c0, c1)
 
-        load_scales(l_scale_raw[0], ref_bra_scales, 0)
         load_words(l_raw[0], ref_bra_words, 0, 0, 2)
         load_words(r_words[0], ref_ket_words, 0, 0, 2)
+        zero(nc.vector, l_scale_raw[0])
         zero(nc.vector, r_scale[0])
-        nc.vector.memset(l_scale[0][:].rearrange("p t e n -> p (t e n)").bitcast(I32), 0)
-        nc.vector.memset(ident[:], 0.0)
-        make_identity(nc, ident[:], nomemset=True)
         zero(nc.vector, r_scale[1])
         zero(nc.vector, l_scale_raw[1])
 
+        load_scales(l_scale_raw[0], ref_bra_scales, 0)
         load_scales(r_scale[0], ref_ket_scales, 0)
         load_words(l_raw[0], ref_bra_words, 0, 2, 4)
         load_words(r_words[0], ref_ket_words, 0, 2, 4)
@@ -308,14 +298,13 @@ def tile_two_copy_overlap_s12_kernel(
         load_rows("bra", 3)
         load_coh(1)
 
-        order_l_scale_rows(0, 0, 2)
         order_l_words(0, 0, 2)
-        order_l_scale_rows(0, 2, 4)
+        order_l_scales(0)
+        nc.vector.memset(ident[:], 0.0)
+        make_identity(nc, ident[:], nomemset=True)
         order_l_words(0, 2, 4)
-        nc.scalar.activation(
-            out=perm[:].rearrange("k (t p j) -> k t p j", t=4, j=4),
-            in_=ident[:].rearrange("k (p t j) -> k t p j", t=4, j=4),
-            func=COPY,
+        nc.vector.tensor_copy(
+            out=perm[:].rearrange("k (t p j) -> k t p j", t=4, j=4), in_=ident[:].rearrange("k (p t j) -> k t p j", t=4, j=4)
         )
         nc.scalar.copy(out=filt_col[:], in_=filt_raw[:, :, 0:13:4])
 

@@ -230,6 +230,25 @@ def tile_two_copy_overlap_s12_kernel(
                 paired[g, ch][:].rearrange("p tp c t -> p tp (c t)").bitcast(F32)[:, :, c0:c1].rearrange("p tp c -> p c tp"),
             )
 
+        def warm_up(count):
+            blank = kept("blank", [P, HALF], BF16)
+            blank_codes = kept("blank_codes", [P, HALF], U32)
+            blank_scales = kept("blank_scales", [P, HALF], U8)
+            nc.vector.memset(blank[:], 0.0)
+            nc.vector.memset(blank_codes[:, P:], 0)
+            nc.vector.memset(blank_scales[:].bitcast(U32), 0)
+            nc.vector.quantize_mx(out=blank_codes[:, 0:P].bitcast(FP8X4), scales=blank_scales[:, 0:P], in_=blank[:])
+            for i in range(count):
+                nc.tensor.matmul_mx(
+                    out=banks[7][:],
+                    lhsT=blank_codes[:, 0:P].bitcast(FP8X4),
+                    lhsT_scale=blank_scales[:, 0:P],
+                    rhs=blank_codes[:].bitcast(FP8X4),
+                    rhs_scale=blank_scales[:],
+                    start=True,
+                    stop=True,
+                )
+
         def out_mm(ah, ch, i, c0=0, c1=HALF):
             bank = next_bank()
             held["out", ah, ch, i, c0] = bank
@@ -250,6 +269,29 @@ def tile_two_copy_overlap_s12_kernel(
             copy_on(engine, result[:], held["out", ah, ch, i, c0][:, 0 : c1 - c0])
             row0 = HALF * ah + P * i
             nc.sync.dma_start(out=out[row0 : row0 + P, HALF * ch + c0 : HALF * ch + c1], in_=result[:])
+
+        def out_quarter(engine, cq, pair):
+            bank = next_bank()
+            c_cols = slice(256 * (cq % 2), 256 * (cq % 2 + 1))
+            for s in range(2):
+                ah, i = divmod(2 * pair + s, 4)
+                a_cols = slice(P * i, P * (i + 1))
+                for g in range(2):
+                    nc.tensor.matmul_mx(
+                        out=bank[:, 256 * s : 256 * (s + 1)],
+                        lhsT=q_codes["rho", g, ah][:, a_cols].bitcast(FP8X4),
+                        lhsT_scale=q_scales["rho", g, ah][:, a_cols],
+                        rhs=q_codes["sig", g, cq // 2][:, c_cols].bitcast(FP8X4),
+                        rhs_scale=q_scales["sig", g, cq // 2][:, c_cols],
+                        start=(g == 0),
+                        stop=(g == 1),
+                    )
+            result = stage.tile([P, HALF], F32, name="result", bufs=8, align_bytes=64)
+            copy_on(engine, result[:], bank[:])
+            nc.sync.dma_start(
+                out=out[2 * P * pair : 2 * P * (pair + 1), 256 * cq : 256 * (cq + 1)].rearrange("(s p) c -> p s c", s=2),
+                in_=result[:].rearrange("p (s c) -> p s c", s=2),
+            )
 
         def quant_bra(ch, x):
             quant_turned("bra", ch, HALF * x, HALF * (x + 1))
@@ -274,6 +316,7 @@ def tile_two_copy_overlap_s12_kernel(
         load_words(r_words[0], ref_ket_words, 0, 0, 2)
         zero(nc.vector, l_scale_raw[0])
         zero(nc.vector, r_scale[0])
+        warm_up(4)
         zero(nc.vector, r_scale[1])
         zero(nc.vector, l_scale_raw[1])
 
@@ -281,28 +324,28 @@ def tile_two_copy_overlap_s12_kernel(
         load_scales(r_scale[0], ref_ket_scales, 0)
         load_words(l_raw[0], ref_bra_words, 0, 2, 4)
         load_words(r_words[0], ref_ket_words, 0, 2, 4)
+        load_scales(r_scale[1], ref_ket_scales, 1)
+        load_words(r_words[1], ref_ket_words, 1, 0, 4)
         for j in range(4):
             load_filt(j)
         load_rows("ket", 0)
         load_rows("ket", 1)
-        load_scales(r_scale[1], ref_ket_scales, 1)
-        load_words(r_words[1], ref_ket_words, 1, 0, 4)
-        load_rows("ket", 2)
-        load_rows("ket", 3)
         load_scales(l_scale_raw[1], ref_bra_scales, 1)
         load_words(l_raw[1], ref_bra_words, 1, 0, 4)
+        load_rows("ket", 2)
+        load_rows("ket", 3)
         load_rows("bra", 0)
         load_rows("bra", 1)
         load_coh(0)
+        load_coh(1)
         load_rows("bra", 2)
         load_rows("bra", 3)
-        load_coh(1)
 
         order_l_words(0, 0, 2)
         order_l_scales(0)
+        order_l_words(0, 2, 4)
         nc.vector.memset(ident[:], 0.0)
         make_identity(nc, ident[:], nomemset=True)
-        order_l_words(0, 2, 4)
         nc.vector.tensor_copy(
             out=perm[:].rearrange("k (t p j) -> k t p j", t=4, j=4), in_=ident[:].rearrange("k (p t j) -> k t p j", t=4, j=4)
         )
@@ -321,85 +364,84 @@ def tile_two_copy_overlap_s12_kernel(
             for e in range(2, 4):
                 rho_pass(held["rho", 0, 0, t], 0, 0, t, e)
             rho_out(0, 0, t)
-        order_rows("ket", 0, "dve")
-        order_rows("ket", 1, "dve")
-        turn_run("ket", 0, ("dve", "dve", "act", "act"))
-        weave("rho", 0, 0)
         rho(0, 1, 0)
-        order_rows("ket", 2, "act")
+        order_rows("ket", 0, "dve")
+        weave("rho", 0, 0)
         rho(0, 1, 1)
-        order_rows("ket", 3, "dve")
-        quant_woven("rho", 0, 0)
-        quant_turned("ket", 0, 0, 2 * HALF)
+        order_rows("ket", 1, "dve")
         rho(0, 1, 2)
-        rho(0, 1, 3)
         order_l_scales(1)
+        rho(0, 1, 3)
         order_l_words(1, 0, 4)
-        turn_run("ket", 1, ("act", "act", "act", "act"))
-        order_rows("bra", 0, "dve")
+        turn_run("ket", 0, ("act", "act", "act", "act"))
+        quant_woven("rho", 0, 0)
         weave("rho", 0, 1)
-        order_rows("bra", 1, "dve")
+        order_rows("ket", 2, "dve")
         rho(1, 0, 0)
-        rho(1, 0, 1)
         quant_woven("rho", 0, 1)
+        order_rows("ket", 3, "dve")
+        rho(1, 0, 1)
+        quant_turned("ket", 0, 0, 2 * HALF)
+        rho(1, 0, 2)
+        order_rows("bra", 0, "dve")
+        order_rows("bra", 1, "dve")
+        turn_run("ket", 1, ("act", "act", "act", "dve"))
+        rho(1, 0, 3)
         quant_turned("ket", 1, 0, 2 * HALF)
         turn_run("bra", 0, ("act", "act", "act", "act"))
-        order_rows("bra", 2, "dve")
-        rho(1, 0, 2)
+        weave("rho", 1, 0, 0, 256)
         quant_bra(0, 0)
-        order_rows("bra", 3, "dve")
-        rho(1, 0, 3)
         quant_bra(0, 1)
+        weave("rho", 1, 0, 256, HALF)
         rho(1, 1, 0)
-        weave("rho", 1, 0)
-        sig(0, 0, 0)
-        sig(0, 0, 1)
-        turn_run("bra", 1, ("act", "act", "act", "act"))
-        quant_woven("rho", 1, 0)
-        sig(0, 0, 2)
-        sig(0, 0, 3)
         rho(1, 1, 1)
-        quant_bra(1, 0)
+        for j in range(4):
+            sig(0, 0, j)
+        order_rows("bra", 2, "act")
+        order_rows("bra", 3, "act")
         weave_sig(0, 0, 0, HALF, "act")
         sig(1, 0, 0)
+        quant_woven("rho", 1, 0)
         sig(1, 0, 1)
-        quant_bra(1, 1)
-        rho(1, 1, 2)
-        weave_sig(1, 0, 0, 256, "act")
-        quant_woven("sig", 0, 0)
         sig(1, 0, 2)
         sig(1, 0, 3)
+        quant_woven("sig", 0, 0)
+        rho(1, 1, 2)
+        weave_sig(1, 0)
+        turn_run("bra", 1, ("act", "act", "act", "act"))
+        quant_woven("sig", 1, 0)
+        quant_bra(1, 0)
         rho(1, 1, 3)
-        quant_woven("sig", 1, 0, 0, 256)
-        weave_sig(1, 0, 256, HALF)
-        sig_mm(0, 1, 0)
-        quant_woven("sig", 1, 0, 256, HALF)
-        sig_out(0, 1, 0)
-        weave("rho", 1, 1, 0, HALF, "act")
-        sig(0, 1, 1)
-        sig(0, 1, 2)
+        quant_bra(1, 1)
+        weave("rho", 1, 1)
         outg("act", 0, 0, 0)
-        sig(0, 1, 3)
+        sig(0, 1, 0)
         outg("act", 0, 0, 1)
-        sig(1, 1, 0)
+        sig(0, 1, 1)
         quant_woven("rho", 1, 1)
-        weave_sig(0, 1, 0, HALF, "act")
         outg("act", 0, 0, 2)
-        sig(1, 1, 1)
-        weave_sig(1, 1, 0, 256, "act")
-        sig(1, 1, 2)
+        weave_sig(0, 1, 0, 256, "act")
+        sig(1, 1, 0)
         outg("act", 0, 0, 3)
-        sig(1, 1, 3)
-        quant_woven("sig", 0, 1)
-        weave_sig(1, 1, 256, HALF)
+        sig(1, 1, 1)
+        quant_woven("sig", 0, 1, 0, 256)
+        outg("act", 1, 0, 0)
+        weave_sig(1, 1, 0, 256, "act")
+        sig(0, 1, 2)
+        outg("act", 1, 0, 1)
+        sig(0, 1, 3)
         quant_woven("sig", 1, 1, 0, 256)
+        outg("act", 1, 0, 2)
+        weave_sig(0, 1, 256, HALF, "act")
+        sig(1, 1, 2)
+        outg("act", 1, 0, 3)
+        sig(1, 1, 3)
+        quant_woven("sig", 0, 1, 256, HALF)
+        weave_sig(1, 1, 256, HALF)
         quant_woven("sig", 1, 1, 256, HALF)
-        for i in range(4):
-            outg("act", 1, 0, i)
-        for ah in range(2):
-            for i in range(4):
-                if ah == 1 and i == 3:
-                    outg("act", 1, 1, 3, 0, 256)
-                    outg("dve", 1, 1, 3, 256, HALF)
-                else:
-                    outg("dve" if i % 2 == 0 else "act", ah, 1, i)
+        for pair in range(4):
+            out_quarter("act", 2, pair)
+        for pair in range(3):
+            out_quarter("dve" if pair % 2 == 0 else "act", 3, pair)
+        outg("act", 1, 1, 2, 256, HALF)
+        outg("dve", 1, 1, 3, 256, HALF)

@@ -41,8 +41,9 @@ def tile_two_copy_overlap_s12_kernel(
 
         ident = kept("ident", [P, P], F32)
         perm = kept("perm", [P, P], F32)
-        filt_raw = kept("filt_raw", [P, 2, 16], BF16)
-        filt_col = kept("filt_col", [P, 2, 4], F32)
+        filt_raw = kept("filt_raw", [P, 256], BF16)
+        filt_sorted = kept("filt_sorted", [P, 256], F32)
+        filt_col = kept("filt_col", [P, 256], F32)
         rows = {(w, j): kept("%s_rows%d" % (w, j), [P, 2, F], BF16) for w in ("ket", "bra") for j in range(4)}
         turned = {(w, g): kept("%s_turned%d" % (w, g), [P, 2 * HALF * 4], BF16) for w in ("ket", "bra") for g in range(2)}
         codes = {(w, g): kept("%s_codes%d" % (w, g), [P, 2 * HALF], U32) for w in ("ket", "bra") for g in range(2)}
@@ -63,10 +64,10 @@ def tile_two_copy_overlap_s12_kernel(
             src = ket if w == "ket" else bra
             nc.sync.dma_start(out=rows[w, j][:], in_=src[2 * j * P : 2 * (j + 1) * P, :].rearrange("(s p) f -> p s f", s=2))
 
-        def load_scales(plane, src, h, r0=0, r1=4):
+        def load_scales(plane, src, h, r0=0, r1=4, queue=nc.sync):
             by_row = src.bitcast(I32).rearrange("e (q r) n -> r q e n", r=4)
             for r in range(r0, r1):
-                nc.sync.dma_start(out=plane[r:P:32, :, :].bitcast(I32), in_=by_row[r][:, :, h * P : (h + 1) * P])
+                queue.dma_start(out=plane[r:P:32, :, :].bitcast(I32), in_=by_row[r][:, :, h * P : (h + 1) * P])
 
         def load_words(tile, src, h, e0, e1, queue=nc.sync):
             view = src.bitcast(I32).rearrange("e p n -> p e n")
@@ -77,9 +78,17 @@ def tile_two_copy_overlap_s12_kernel(
             for j in range(4):
                 nc.sync.dma_start(out=coh_sb[g][j:P:4, :, :], in_=view[g][j])
 
-        def load_filt(j):
-            by_16 = filt.rearrange("(g p s) -> p g s", g=2, s=16)
-            nc.sync.dma_start(out=filt_raw[j:P:4, :, 0:13], in_=by_16[:, :, j : j + 13])
+        def load_filt():
+            nc.sync.dma_start(
+                out=filt_raw[0:P:32, :].rearrange("q (g n) -> q g n", g=2), in_=filt.rearrange("(g q n) -> q g n", g=2, q=4)
+            )
+
+        def spread_filt():
+            nc.vector.tensor_copy(
+                out=filt_sorted[:].rearrange("q (g t x j) -> q g t x j", g=2, t=4, j=4),
+                in_=filt_raw[:].rearrange("q (g x t j) -> q g t x j", g=2, t=4, j=4),
+            )
+            nc.vector.transpose(out=filt_col[:], in_=filt_sorted[:])
 
         def zero(engine, plane):
             engine.memset(plane[:].rearrange("p e n -> p (e n)").bitcast(I32), 0)
@@ -170,7 +179,7 @@ def tile_two_copy_overlap_s12_kernel(
             bank = held["rho", g, ah, t]
             if t == 0:
                 flat["rho", g, ah] = stage.tile([P, 4, HALF], BF16, name="rho_flat", bufs=3, align_bytes=64)
-            nc.scalar.activation(out=flat["rho", g, ah][:, t, c0:c1], in_=bank[:, c0:c1], func=COPY, scale=filt_col[:, g, t : t + 1])
+            nc.scalar.activation(out=flat["rho", g, ah][:, t, c0:c1], in_=bank[:, c0:c1], func=COPY, scale=filt_col[:, 32 * (4 * g + t) : 32 * (4 * g + t) + 1])
 
         def weave(w, g, ah, c0=0, c1=HALF, engine="dve"):
             if c0 == 0:
@@ -231,20 +240,13 @@ def tile_two_copy_overlap_s12_kernel(
             )
 
         def warm_up(count):
-            blank = kept("blank", [P, HALF], BF16)
-            blank_codes = kept("blank_codes", [P, HALF], U32)
-            blank_scales = kept("blank_scales", [P, HALF], U8)
-            nc.vector.memset(blank[:], 0.0)
-            nc.vector.memset(blank_codes[:, P:], 0)
-            nc.vector.memset(blank_scales[:].bitcast(U32), 0)
-            nc.vector.quantize_mx(out=blank_codes[:, 0:P].bitcast(FP8X4), scales=blank_scales[:, 0:P], in_=blank[:])
             for i in range(count):
                 nc.tensor.matmul_mx(
                     out=banks[7][:],
-                    lhsT=blank_codes[:, 0:P].bitcast(FP8X4),
-                    lhsT_scale=blank_scales[:, 0:P],
-                    rhs=blank_codes[:].bitcast(FP8X4),
-                    rhs_scale=blank_scales[:],
+                    lhsT=l_raw[0][:, 0, 0 : 2 * P].bitcast(FP4X4),
+                    lhsT_scale=l_scale_raw[1][:, 0, 0:P],
+                    rhs=l_raw[0][:, 0, :].bitcast(FP4X4),
+                    rhs_scale=l_scale_raw[1][:, 0, :],
                     start=True,
                     stop=True,
                 )
@@ -314,20 +316,21 @@ def tile_two_copy_overlap_s12_kernel(
 
         load_words(l_raw[0], ref_bra_words, 0, 0, 2)
         load_words(r_words[0], ref_ket_words, 0, 0, 2)
-        zero(nc.vector, l_scale_raw[0])
         zero(nc.vector, r_scale[0])
-        warm_up(4)
-        zero(nc.vector, r_scale[1])
+        zero(nc.vector, l_scale_raw[0])
         zero(nc.vector, l_scale_raw[1])
-
         load_scales(l_scale_raw[0], ref_bra_scales, 0)
-        load_scales(r_scale[0], ref_ket_scales, 0)
+        load_scales(r_scale[0], ref_ket_scales, 0, 0, 2)
+        load_scales(r_scale[0], ref_ket_scales, 0, 2, 4, nc.gpsimd)
+        warm_up(4)
+        order_l_words(0, 0, 2)
+        zero(nc.vector, r_scale[1])
+        nc.vector.memset(filt_raw[:], 0.0)
         load_words(l_raw[0], ref_bra_words, 0, 2, 4)
         load_words(r_words[0], ref_ket_words, 0, 2, 4)
+        load_filt()
         load_scales(r_scale[1], ref_ket_scales, 1)
         load_words(r_words[1], ref_ket_words, 1, 0, 4)
-        for j in range(4):
-            load_filt(j)
         load_rows("ket", 0)
         load_rows("ket", 1)
         load_scales(l_scale_raw[1], ref_bra_scales, 1)
@@ -341,15 +344,14 @@ def tile_two_copy_overlap_s12_kernel(
         load_rows("bra", 2)
         load_rows("bra", 3)
 
-        order_l_words(0, 0, 2)
         order_l_scales(0)
         order_l_words(0, 2, 4)
+        spread_filt()
         nc.vector.memset(ident[:], 0.0)
         make_identity(nc, ident[:], nomemset=True)
         nc.vector.tensor_copy(
             out=perm[:].rearrange("k (t p j) -> k t p j", t=4, j=4), in_=ident[:].rearrange("k (p t j) -> k t p j", t=4, j=4)
         )
-        nc.scalar.copy(out=filt_col[:], in_=filt_raw[:, :, 0:13:4])
 
         def turn_run(w, half, engines):
             for j in range(4):

@@ -145,10 +145,10 @@ def tile_two_copy_overlap_s12_kernel(
                 in_=turned[w, g][:, 4 * c0 : 4 * c1],
             )
 
-        def order_l_scales(g):
+        def order_l_scales(g, e0=0, e1=4):
             nc.vector.tensor_copy(
-                out=l_scale[g][:].rearrange("k t e n -> k t (e n)").bitcast(I32),
-                in_=l_scale_raw[g][:].rearrange("k e n -> k (e n)").bitcast(I32).rearrange("k (x t) -> k t x", t=4),
+                out=l_scale[g][:, :, e0:e1, :].rearrange("k t e n -> k t (e n)").bitcast(I32).rearrange("k t (b i) -> k b t i", i=4),
+                in_=l_scale_raw[g][:, e0:e1, :].rearrange("k e n -> k (e n)").bitcast(I32).rearrange("k (b i t) -> k b t i", i=4, t=4),
             )
 
         def order_l_words(g, e0, e1):
@@ -239,14 +239,14 @@ def tile_two_copy_overlap_s12_kernel(
                 paired[g, ch][:].rearrange("p tp c t -> p tp (c t)").bitcast(F32)[:, :, c0:c1].rearrange("p tp c -> p c tp"),
             )
 
-        def warm_up(count):
+        def warm_up(count, plane):
             for i in range(count):
                 nc.tensor.matmul_mx(
                     out=banks[7][:],
                     lhsT=l_raw[0][:, 0, 0 : 2 * P].bitcast(FP4X4),
-                    lhsT_scale=l_scale_raw[1][:, 0, 0:P],
+                    lhsT_scale=plane[:, 0, 0:P],
                     rhs=l_raw[0][:, 0, :].bitcast(FP4X4),
-                    rhs_scale=l_scale_raw[1][:, 0, :],
+                    rhs_scale=plane[:, 0, :],
                     start=True,
                     stop=True,
                 )
@@ -322,7 +322,8 @@ def tile_two_copy_overlap_s12_kernel(
         load_scales(l_scale_raw[0], ref_bra_scales, 0)
         load_scales(r_scale[0], ref_ket_scales, 0, 0, 2)
         load_scales(r_scale[0], ref_ket_scales, 0, 2, 4, nc.gpsimd)
-        warm_up(4)
+        warm_up(3, l_scale_raw[1])
+        warm_up(2, l_scale_raw[0])
         order_l_words(0, 0, 2)
         zero(nc.vector, r_scale[1])
         nc.vector.memset(filt_raw[:], 0.0)
@@ -344,7 +345,8 @@ def tile_two_copy_overlap_s12_kernel(
         load_rows("bra", 2)
         load_rows("bra", 3)
 
-        order_l_scales(0)
+        order_l_scales(0, 0, 2)
+        order_l_scales(0, 2, 4)
         order_l_words(0, 2, 4)
         spread_filt()
         nc.vector.memset(ident[:], 0.0)
@@ -373,44 +375,41 @@ def tile_two_copy_overlap_s12_kernel(
         order_rows("ket", 1, "dve")
         rho(0, 1, 2)
         order_l_scales(1)
-        rho(0, 1, 3)
+        quant_woven("rho", 0, 0)
         order_l_words(1, 0, 4)
         turn_run("ket", 0, ("act", "act", "act", "act"))
-        quant_woven("rho", 0, 0)
-        weave("rho", 0, 1)
+        rho(0, 1, 3)
         order_rows("ket", 2, "dve")
-        rho(1, 0, 0)
-        quant_woven("rho", 0, 1)
-        order_rows("ket", 3, "dve")
-        rho(1, 0, 1)
         quant_turned("ket", 0, 0, 2 * HALF)
-        rho(1, 0, 2)
+        order_rows("ket", 3, "dve")
+        rho(1, 0, 0)
+        weave("rho", 0, 1)
+        rho(1, 0, 1)
         order_rows("bra", 0, "dve")
         order_rows("bra", 1, "dve")
-        turn_run("ket", 1, ("act", "act", "act", "dve"))
-        rho(1, 0, 3)
+        turn_run("ket", 1, ("act", "act", "act", "act"))
+        quant_woven("rho", 0, 1)
+        rho(1, 0, 2)
         quant_turned("ket", 1, 0, 2 * HALF)
         turn_run("bra", 0, ("act", "act", "act", "act"))
-        weave("rho", 1, 0, 0, 256)
         quant_bra(0, 0)
         quant_bra(0, 1)
-        weave("rho", 1, 0, 256, HALF)
+        rho(1, 0, 3)
         rho(1, 1, 0)
-        rho(1, 1, 1)
+        weave("rho", 1, 0)
         for j in range(4):
             sig(0, 0, j)
         order_rows("bra", 2, "act")
         order_rows("bra", 3, "act")
-        weave_sig(0, 0, 0, HALF, "act")
-        sig(1, 0, 0)
+        rho(1, 1, 1)
         quant_woven("rho", 1, 0)
-        sig(1, 0, 1)
-        sig(1, 0, 2)
-        sig(1, 0, 3)
+        weave_sig(0, 0, 0, HALF, "act")
+        for j in range(4):
+            sig(1, 0, j)
         quant_woven("sig", 0, 0)
-        rho(1, 1, 2)
         weave_sig(1, 0)
         turn_run("bra", 1, ("act", "act", "act", "act"))
+        rho(1, 1, 2)
         quant_woven("sig", 1, 0)
         quant_bra(1, 0)
         rho(1, 1, 3)

@@ -233,11 +233,16 @@ def tile_two_copy_overlap_s12_kernel(
         def weave_sig(g, ch, c0=0, c1=HALF, engine="dve"):
             if c0 == 0:
                 woven["sig", g, ch] = stage.tile([P, HALF * 4], BF16, name="woven", bufs=4, align_bytes=64)
-            copy_on(
-                engine,
-                woven["sig", g, ch][:, 4 * c0 : 4 * c1].bitcast(F32).rearrange("p (c tp) -> p c tp", tp=2),
-                paired[g, ch][:].rearrange("p tp c t -> p tp (c t)").bitcast(F32)[:, :, c0:c1].rearrange("p tp c -> p c tp"),
-            )
+            if engine == "act":
+                nc.scalar.copy(
+                    out=woven["sig", g, ch][:, 4 * c0 : 4 * c1].rearrange("p (c tp t) -> p c tp t", tp=2, t=2),
+                    in_=paired[g, ch][:, :, c0:c1, :].rearrange("p tp c t -> p c tp t"),
+                )
+            else:
+                nc.vector.tensor_copy(
+                    out=woven["sig", g, ch][:, 4 * c0 : 4 * c1].bitcast(F32).rearrange("p (c tp) -> p c tp", tp=2),
+                    in_=paired[g, ch][:].rearrange("p tp c t -> p tp (c t)").bitcast(F32)[:, :, c0:c1].rearrange("p tp c -> p c tp"),
+                )
 
         def warm_up(count, plane):
             for i in range(count):
@@ -320,8 +325,8 @@ def tile_two_copy_overlap_s12_kernel(
         zero(nc.vector, l_scale_raw[0])
         zero(nc.vector, l_scale_raw[1])
         load_scales(l_scale_raw[0], ref_bra_scales, 0)
-        load_scales(r_scale[0], ref_ket_scales, 0, 0, 2)
-        load_scales(r_scale[0], ref_ket_scales, 0, 2, 4, nc.gpsimd)
+        load_scales(r_scale[0], ref_ket_scales, 0, 0, 3)
+        load_scales(r_scale[0], ref_ket_scales, 0, 3, 4, nc.gpsimd)
         warm_up(3, l_scale_raw[1])
         warm_up(2, l_scale_raw[0])
         order_l_words(0, 0, 2)
@@ -377,11 +382,15 @@ def tile_two_copy_overlap_s12_kernel(
         order_l_scales(1)
         quant_woven("rho", 0, 0)
         order_l_words(1, 0, 4)
-        turn_run("ket", 0, ("act", "act", "act", "act"))
-        rho(0, 1, 3)
+        for j in range(4):
+            turn_mm("ket", j)
+        for j in range(3):
+            turn_out("ket", j, "act")
         order_rows("ket", 2, "dve")
-        quant_turned("ket", 0, 0, 2 * HALF)
+        turn_out("ket", 3, "dve")
+        rho(0, 1, 3)
         order_rows("ket", 3, "dve")
+        quant_turned("ket", 0, 0, 2 * HALF)
         rho(1, 0, 0)
         weave("rho", 0, 1)
         rho(1, 0, 1)
@@ -396,11 +405,11 @@ def tile_two_copy_overlap_s12_kernel(
         quant_bra(0, 1)
         rho(1, 0, 3)
         rho(1, 1, 0)
-        weave("rho", 1, 0)
+        weave("rho", 1, 0, 0, HALF, "act")
+        order_rows("bra", 2, "dve")
         for j in range(4):
             sig(0, 0, j)
-        order_rows("bra", 2, "act")
-        order_rows("bra", 3, "act")
+        order_rows("bra", 3, "dve")
         rho(1, 1, 1)
         quant_woven("rho", 1, 0)
         weave_sig(0, 0, 0, HALF, "act")
@@ -410,15 +419,15 @@ def tile_two_copy_overlap_s12_kernel(
         weave_sig(1, 0)
         turn_run("bra", 1, ("act", "act", "act", "act"))
         rho(1, 1, 2)
-        quant_woven("sig", 1, 0)
         quant_bra(1, 0)
+        quant_woven("sig", 1, 0)
         rho(1, 1, 3)
         quant_bra(1, 1)
         weave("rho", 1, 1)
-        outg("act", 0, 0, 0)
         sig(0, 1, 0)
-        outg("act", 0, 0, 1)
+        outg("act", 0, 0, 0)
         sig(0, 1, 1)
+        outg("act", 0, 0, 1)
         quant_woven("rho", 1, 1)
         outg("act", 0, 0, 2)
         weave_sig(0, 1, 0, 256, "act")
@@ -433,8 +442,8 @@ def tile_two_copy_overlap_s12_kernel(
         sig(0, 1, 3)
         quant_woven("sig", 1, 1, 0, 256)
         outg("act", 1, 0, 2)
-        weave_sig(0, 1, 256, HALF, "act")
         sig(1, 1, 2)
+        weave_sig(0, 1, 256, HALF)
         outg("act", 1, 0, 3)
         sig(1, 1, 3)
         quant_woven("sig", 0, 1, 256, HALF)

@@ -48,11 +48,13 @@ def tile_two_copy_overlap_s12_kernel(
         turned = {(w, g): kept("%s_turned%d" % (w, g), [P, 2 * HALF * 4], BF16) for w in ("ket", "bra") for g in range(2)}
         codes = {(w, g): kept("%s_codes%d" % (w, g), [P, 2 * HALF], U32) for w in ("ket", "bra") for g in range(2)}
         scales = {(w, g): kept("%s_scales%d" % (w, g), [P, 2 * HALF], U8) for w in ("ket", "bra") for g in range(2)}
-        l_raw = [kept("l_raw%d" % g, [P, 4, 2 * HALF], U8) for g in range(2)]
-        l_words = [kept("l_words%d" % g, [P, 4, 4, 2 * P], U8) for g in range(2)]
+        pieces = [(0, 0, 2), (0, 2, 4), (1, 0, 4)]
+        first_pass = {(h, e): e0 for h, e0, e1 in pieces for e in range(e0, e1)}
+        l_raw = {(g, e0): kept("l_raw%d%d" % (g, e0), [P, e1 - e0, 2 * HALF], U8) for g, e0, e1 in pieces}
+        l_words = {(g, e0): kept("l_words%d%d" % (g, e0), [P, 4, e1 - e0, 2 * P], U8) for g, e0, e1 in pieces}
         l_scale_raw = [kept("l_scale_raw%d" % g, [P, 4, HALF], U8) for g in range(2)]
         l_scale = [kept("l_scale%d" % g, [P, 4, 4, P], U8) for g in range(2)]
-        r_words = [kept("r_words%d" % h, [P, 4, 2 * HALF], U8) for h in range(2)]
+        r_words = {(h, e0): kept("r_words%d%d" % (h, e0), [P, e1 - e0, 2 * HALF], U8) for h, e0, e1 in pieces}
         r_scale = [kept("r_scale%d" % h, [P, 4, HALF], U8) for h in range(2)]
         coh_sb = [kept("coh%d" % g, [P, 4, A], BF16) for g in range(2)]
         q_codes = {(w, g, h): kept("%s_q%d%d" % (w, g, h), [P, HALF], U32) for w in ("rho", "sig") for g in range(2) for h in range(2)}
@@ -69,9 +71,9 @@ def tile_two_copy_overlap_s12_kernel(
             for r in range(r0, r1):
                 queue.dma_start(out=plane[r:P:32, :, :].bitcast(I32), in_=by_row[r][:, :, h * P : (h + 1) * P])
 
-        def load_words(tile, src, h, e0, e1, queue=nc.sync):
+        def load_words(tiles, src, h, e0, e1):
             view = src.bitcast(I32).rearrange("e p n -> p e n")
-            queue.dma_start(out=tile[:, e0:e1, :].bitcast(I32), in_=view[:, e0:e1, h * 256 : (h + 1) * 256])
+            nc.sync.dma_start(out=tiles[h, e0][:].bitcast(I32), in_=view[:, e0:e1, h * 256 : (h + 1) * 256])
 
         def load_coh(g):
             view = coh.rearrange("(g p t j) c -> g j p t c", g=2, t=4, j=4)
@@ -151,18 +153,18 @@ def tile_two_copy_overlap_s12_kernel(
                 in_=l_scale_raw[g][:, e0:e1, :].rearrange("k e n -> k (e n)").bitcast(I32).rearrange("k (b i t) -> k b t i", i=4, t=4),
             )
 
-        def order_l_words(g, e0, e1):
+        def order_l_words(g, e0):
             nc.vector.tensor_copy(
-                out=l_words[g][:, :, e0:e1, :].rearrange("k t e n -> k t (e n)").bitcast(I32).rearrange("k t (x w) -> k t x w", w=2),
-                in_=l_raw[g][:, e0:e1, :].rearrange("k e n -> k (e n)").bitcast(I32).rearrange("k (x t w) -> k t x w", t=4, w=2),
+                out=l_words[g, e0][:].rearrange("k t e n -> k t (e n)").bitcast(I32).rearrange("k t (x w) -> k t x w", w=2),
+                in_=l_raw[g, e0][:].rearrange("k e n -> k (e n)").bitcast(I32).rearrange("k (x t w) -> k t x w", t=4, w=2),
             )
 
         def rho_pass(bank, g, ah, t, e):
             nc.tensor.matmul_mx(
                 out=bank[:],
-                lhsT=l_words[g][:, t, e, :].bitcast(FP4X4),
+                lhsT=l_words[g, first_pass[g, e]][:, t, e - first_pass[g, e], :].bitcast(FP4X4),
                 lhsT_scale=l_scale[g][:, t, e, :],
-                rhs=r_words[ah][:, e, :].bitcast(FP4X4),
+                rhs=r_words[ah, first_pass[ah, e]][:, e - first_pass[ah, e], :].bitcast(FP4X4),
                 rhs_scale=r_scale[ah][:, e, :],
                 start=(e == 0),
                 stop=(e == 3),
@@ -248,9 +250,9 @@ def tile_two_copy_overlap_s12_kernel(
             for i in range(count):
                 nc.tensor.matmul_mx(
                     out=banks[7][:],
-                    lhsT=l_raw[0][:, 0, 0 : 2 * P].bitcast(FP4X4),
+                    lhsT=l_raw[0, 0][:, 0, 0 : 2 * P].bitcast(FP4X4),
                     lhsT_scale=plane[:, 0, 0:P],
-                    rhs=l_raw[0][:, 0, :].bitcast(FP4X4),
+                    rhs=l_raw[0, 0][:, 0, :].bitcast(FP4X4),
                     rhs_scale=plane[:, 0, :],
                     start=True,
                     stop=True,
@@ -319,28 +321,33 @@ def tile_two_copy_overlap_s12_kernel(
             out_mm(ah, ch, i, c0, c1)
             out_store(engine, ah, ch, i, c0, c1)
 
-        load_words(l_raw[0], ref_bra_words, 0, 0, 2)
-        load_words(r_words[0], ref_ket_words, 0, 0, 2)
+        load_words(l_raw, ref_bra_words, 0, 0, 2)
+        load_words(r_words, ref_ket_words, 0, 0, 2)
         zero(nc.vector, r_scale[0])
         zero(nc.vector, l_scale_raw[0])
         zero(nc.vector, l_scale_raw[1])
         load_scales(l_scale_raw[0], ref_bra_scales, 0)
         load_scales(r_scale[0], ref_ket_scales, 0, 0, 3)
         load_scales(r_scale[0], ref_ket_scales, 0, 3, 4, nc.gpsimd)
+        nc.vector.memset(ident[:], 0.0)
+        make_identity(nc, ident[:], nomemset=True)
+        nc.scalar.activation(
+            out=perm[:].rearrange("k (t p j) -> k t p j", t=4, j=4), in_=ident[:].rearrange("k (p t j) -> k t p j", t=4, j=4), func=COPY
+        )
         warm_up(3, l_scale_raw[1])
         warm_up(2, l_scale_raw[0])
-        order_l_words(0, 0, 2)
+        order_l_words(0, 0)
         zero(nc.vector, r_scale[1])
         nc.vector.memset(filt_raw[:], 0.0)
-        load_words(l_raw[0], ref_bra_words, 0, 2, 4)
-        load_words(r_words[0], ref_ket_words, 0, 2, 4)
+        load_words(l_raw, ref_bra_words, 0, 2, 4)
+        load_words(r_words, ref_ket_words, 0, 2, 4)
         load_filt()
         load_scales(r_scale[1], ref_ket_scales, 1)
-        load_words(r_words[1], ref_ket_words, 1, 0, 4)
+        load_words(r_words, ref_ket_words, 1, 0, 4)
         load_rows("ket", 0)
         load_rows("ket", 1)
         load_scales(l_scale_raw[1], ref_bra_scales, 1)
-        load_words(l_raw[1], ref_bra_words, 1, 0, 4)
+        load_words(l_raw, ref_bra_words, 1, 0, 4)
         load_rows("ket", 2)
         load_rows("ket", 3)
         load_rows("bra", 0)
@@ -352,13 +359,8 @@ def tile_two_copy_overlap_s12_kernel(
 
         order_l_scales(0, 0, 2)
         order_l_scales(0, 2, 4)
-        order_l_words(0, 2, 4)
+        order_l_words(0, 2)
         spread_filt()
-        nc.vector.memset(ident[:], 0.0)
-        make_identity(nc, ident[:], nomemset=True)
-        nc.vector.tensor_copy(
-            out=perm[:].rearrange("k (t p j) -> k t p j", t=4, j=4), in_=ident[:].rearrange("k (p t j) -> k t p j", t=4, j=4)
-        )
 
         def turn_run(w, half, engines):
             for j in range(4):
@@ -381,7 +383,7 @@ def tile_two_copy_overlap_s12_kernel(
         rho(0, 1, 2)
         order_l_scales(1)
         quant_woven("rho", 0, 0)
-        order_l_words(1, 0, 4)
+        order_l_words(1, 0)
         for j in range(4):
             turn_mm("ket", j)
         for j in range(3):

@@ -48,7 +48,7 @@ def tile_two_copy_overlap_s12_kernel(
         turned = {(w, g): kept("%s_turned%d" % (w, g), [P, 2 * HALF * 4], BF16) for w in ("ket", "bra") for g in range(2)}
         codes = {(w, g): kept("%s_codes%d" % (w, g), [P, 2 * HALF], U32) for w in ("ket", "bra") for g in range(2)}
         scales = {(w, g): kept("%s_scales%d" % (w, g), [P, 2 * HALF], U8) for w in ("ket", "bra") for g in range(2)}
-        pieces = [(0, 0, 2), (0, 2, 4), (1, 0, 4)]
+        pieces = [(0, 0, 1), (0, 1, 2), (0, 2, 4), (1, 0, 4)]
         first_pass = {(h, e): e0 for h, e0, e1 in pieces for e in range(e0, e1)}
         l_raw = {(g, e0): kept("l_raw%d%d" % (g, e0), [P, e1 - e0, 2 * HALF], U8) for g, e0, e1 in pieces}
         l_words = {(g, e0): kept("l_words%d%d" % (g, e0), [P, 4, e1 - e0, 2 * P], U8) for g, e0, e1 in pieces}
@@ -321,13 +321,14 @@ def tile_two_copy_overlap_s12_kernel(
             out_mm(ah, ch, i, c0, c1)
             out_store(engine, ah, ch, i, c0, c1)
 
-        load_words(l_raw, ref_bra_words, 0, 0, 2)
-        load_words(r_words, ref_ket_words, 0, 0, 2)
+        load_words(l_raw, ref_bra_words, 0, 0, 1)
+        load_words(r_words, ref_ket_words, 0, 0, 1)
         zero(nc.vector, r_scale[0])
         zero(nc.vector, l_scale_raw[0])
         zero(nc.vector, l_scale_raw[1])
+        load_scales(r_scale[0], ref_ket_scales, 0, 0, 2)
         load_scales(l_scale_raw[0], ref_bra_scales, 0)
-        load_scales(r_scale[0], ref_ket_scales, 0, 0, 3)
+        load_scales(r_scale[0], ref_ket_scales, 0, 2, 3)
         load_scales(r_scale[0], ref_ket_scales, 0, 3, 4, nc.gpsimd)
         nc.vector.memset(ident[:], 0.0)
         make_identity(nc, ident[:], nomemset=True)
@@ -335,10 +336,12 @@ def tile_two_copy_overlap_s12_kernel(
             out=perm[:].rearrange("k (t p j) -> k t p j", t=4, j=4), in_=ident[:].rearrange("k (p t j) -> k t p j", t=4, j=4), func=COPY
         )
         warm_up(3, l_scale_raw[1])
-        warm_up(2, l_scale_raw[0])
+        warm_up(1, l_scale_raw[0])
         order_l_words(0, 0)
         zero(nc.vector, r_scale[1])
         nc.vector.memset(filt_raw[:], 0.0)
+        load_words(l_raw, ref_bra_words, 0, 1, 2)
+        load_words(r_words, ref_ket_words, 0, 1, 2)
         load_words(l_raw, ref_bra_words, 0, 2, 4)
         load_words(r_words, ref_ket_words, 0, 2, 4)
         load_filt()
@@ -358,6 +361,7 @@ def tile_two_copy_overlap_s12_kernel(
         load_rows("bra", 3)
 
         order_l_scales(0, 0, 2)
+        order_l_words(0, 1)
         order_l_scales(0, 2, 4)
         order_l_words(0, 2)
         spread_filt()

@@ -45,7 +45,11 @@ def tile_two_copy_overlap_s12_kernel(
         filt_sorted = kept("filt_sorted", [P, 256], F32)
         filt_col = kept("filt_col", [P, 256], F32)
         rows = {(w, j): kept("%s_rows%d" % (w, j), [P, 2, F], BF16) for w in ("ket", "bra") for j in range(4)}
-        turned = {(w, g): kept("%s_turned%d" % (w, g), [P, 2 * HALF * 4], BF16) for w in ("ket", "bra") for g in range(2)}
+        turned = {("ket", g): kept("ket_turned%d" % g, [P, 2 * HALF * 4], BF16) for g in range(2)}
+        for ch in range(2):
+            for x in range(2):
+                turned["bra", ch, x] = kept("bra_turned%d%d" % (ch, x), [P, HALF * 4], BF16)
+        flipped = kept("flipped", [P, 2 * HALF], F32)
         codes = {(w, g): kept("%s_codes%d" % (w, g), [P, 2 * HALF], U32) for w in ("ket", "bra") for g in range(2)}
         scales = {(w, g): kept("%s_scales%d" % (w, g), [P, 2 * HALF], U8) for w in ("ket", "bra") for g in range(2)}
         pieces = [(0, 0, 1), (0, 1, 2), (0, 2, 4), (1, 0, 4)]
@@ -125,27 +129,64 @@ def tile_two_copy_overlap_s12_kernel(
 
         def turn_out(w, j, engine):
             bank = turned_bank[w, j]
-            dst = turned[w, j // 4][:].bitcast(F32)
             jj = j % 4
             if w == "ket":
                 copy_on(
                     engine,
-                    dst.rearrange("p (s jj c u) -> p jj s c u", s=8, jj=4, u=2)[:, jj],
+                    turned[w, j // 4][:].bitcast(F32).rearrange("p (s jj c u) -> p jj s c u", s=8, jj=4, u=2)[:, jj],
                     bank[:].rearrange("p (u s c) -> p s c u", u=2, s=8),
                 )
             else:
                 copy_on(
                     engine,
-                    dst.rearrange("p (jp h j2 c u) -> p jp j2 h c u", jp=2, h=2, j2=2, u=2)[:, jj // 2, jj % 2],
+                    turned[w, j // 4, jj // 2][:].bitcast(F32).rearrange("p (h j2 c u) -> p j2 h c u", h=2, j2=2, u=2)[:, jj % 2],
                     bank[:].rearrange("p (u h c) -> p h c u", u=2, h=2),
                 )
 
-        def quant_turned(w, g, c0, c1):
-            nc.vector.quantize_mx(
-                out=codes[w, g][:, c0:c1].bitcast(FP8X4),
-                scales=scales[w, g][:, c0:c1],
-                in_=turned[w, g][:, 4 * c0 : 4 * c1],
-            )
+        def quant_ket(g):
+            nc.vector.quantize_mx(out=codes["ket", g][:].bitcast(FP8X4), scales=scales["ket", g][:], in_=turned["ket", g][:])
+
+        def quant_bra(ch, x):
+            cols = slice(HALF * x, HALF * (x + 1))
+            nc.vector.quantize_mx(out=codes["bra", ch][:, cols].bitcast(FP8X4), scales=scales["bra", ch][:, cols], in_=turned["bra", ch, x][:])
+
+        def load_quadrants(j):
+            src = bra[2 * j * P : 2 * (j + 1) * P, :].rearrange("(b r) (h q f) -> h q r b f", r=32, h=2, q=4)
+            dst = rows["bra", j][:].rearrange("k h (b f) -> k h b f", b=8)
+            for h in range(2):
+                for q in range(4):
+                    nc.sync.dma_start(out=dst[32 * q : 32 * (q + 1), h], in_=src[h][q])
+
+        def order_quadrants(j, engine):
+            ordered["bra", j] = stage.tile([P, 2 * HALF], F32, name="ordered", bufs=4, align_bytes=64)
+            src = rows["bra", j][:].rearrange("k h f -> k (h f)")
+            if engine == "act":
+                nc.scalar.copy(
+                    out=ordered["bra", j][:].bitcast(BF16).rearrange("k (x u q i) -> k x u q i", u=2, q=4, i=16),
+                    in_=src.rearrange("k (x q u i) -> k x u q i", u=2, q=4, i=16),
+                )
+            else:
+                nc.vector.tensor_copy(
+                    out=ordered["bra", j][:].rearrange("k (x u q i) -> k x u q i", u=2, q=4, i=8),
+                    in_=src.bitcast(F32).rearrange("k (x q u i) -> k x u q i", u=2, q=4, i=8),
+                )
+
+        def flip(j, h):
+            cols = slice(HALF * h, HALF * (h + 1))
+            nc.vector.transpose(out=flipped[:, cols], in_=ordered["bra", j][:, cols])
+
+        def pair_flipped(j, engine):
+            dst = turned["bra", j // 2, j % 2][:]
+            if engine == "act":
+                nc.scalar.copy(
+                    out=dst.rearrange("p (x r u e) -> p x r u e", r=32, u=2, e=2),
+                    in_=flipped[:].bitcast(BF16).rearrange("p (x u r e) -> p x r u e", r=32, u=2, e=2),
+                )
+            else:
+                nc.vector.tensor_copy(
+                    out=dst.bitcast(F32).rearrange("p (x r u) -> p x r u", r=32, u=2),
+                    in_=flipped[:].rearrange("p (x u r) -> p x r u", r=32, u=2),
+                )
 
         def order_l_scales(g, e0=0, e1=4):
             nc.vector.tensor_copy(
@@ -200,6 +241,7 @@ def tile_two_copy_overlap_s12_kernel(
             )
 
         paired = {}
+        woven_sig = {}
 
         def sig_mm(g, ch, jj):
             bank = next_bank()
@@ -222,28 +264,30 @@ def tile_two_copy_overlap_s12_kernel(
 
         def sig_out(g, ch, jj):
             cq, tp = jj // 2, jj % 2
-            if jj == 0:
-                paired[g, ch] = stage.tile([P, 2, HALF, 2], BF16, name="paired", bufs=2, align_bytes=64)
+            if tp == 0:
+                paired[g, ch, cq] = stage.tile([P, 2, 256, 2], BF16, name="paired", bufs=5, align_bytes=64)
             col0 = HALF * ch + 256 * cq
             nc.vector.tensor_tensor(
-                out=paired[g, ch][:, tp, 256 * cq : 256 * (cq + 1), :],
+                out=paired[g, ch, cq][:, tp],
                 in0=held["sig", g, ch, jj][:].rearrange("p (t c) -> p c t", t=2),
                 in1=coh_sb[g][:, 2 * tp : 2 * tp + 2, col0 : col0 + 256].rearrange("p t c -> p c t"),
                 op=MULT,
             )
 
-        def weave_sig(g, ch, c0=0, c1=HALF, engine="dve"):
-            if c0 == 0:
-                woven["sig", g, ch] = stage.tile([P, HALF * 4], BF16, name="woven", bufs=4, align_bytes=64)
+        def weave_sig(g, ch, cq, engine):
+            if (g, ch) not in woven_sig:
+                woven_sig[g, ch] = stage.tile([P, HALF * 4], BF16, name="woven", bufs=4, align_bytes=64)
+                woven["sig", g, ch] = woven_sig[g, ch]
+            dst = woven_sig[g, ch][:, 1024 * cq : 1024 * (cq + 1)]
             if engine == "act":
                 nc.scalar.copy(
-                    out=woven["sig", g, ch][:, 4 * c0 : 4 * c1].rearrange("p (c tp t) -> p c tp t", tp=2, t=2),
-                    in_=paired[g, ch][:, :, c0:c1, :].rearrange("p tp c t -> p c tp t"),
+                    out=dst.rearrange("p (c tp t) -> p c tp t", tp=2, t=2),
+                    in_=paired[g, ch, cq][:].rearrange("p tp c t -> p c tp t"),
                 )
             else:
                 nc.vector.tensor_copy(
-                    out=woven["sig", g, ch][:, 4 * c0 : 4 * c1].bitcast(F32).rearrange("p (c tp) -> p c tp", tp=2),
-                    in_=paired[g, ch][:].rearrange("p tp c t -> p tp (c t)").bitcast(F32)[:, :, c0:c1].rearrange("p tp c -> p c tp"),
+                    out=dst.bitcast(F32).rearrange("p (c tp) -> p c tp", tp=2),
+                    in_=paired[g, ch, cq][:].rearrange("p tp c t -> p tp (c t)").bitcast(F32).rearrange("p tp c -> p c tp"),
                 )
 
         def warm_up(count, plane):
@@ -302,9 +346,6 @@ def tile_two_copy_overlap_s12_kernel(
                 in_=result[:].rearrange("p (s c) -> p s c", s=2),
             )
 
-        def quant_bra(ch, x):
-            quant_turned("bra", ch, HALF * x, HALF * (x + 1))
-
         def rho(g, ah, t):
             rho_mm(g, ah, t)
             rho_out(g, ah, t)
@@ -355,10 +396,10 @@ def tile_two_copy_overlap_s12_kernel(
         load_rows("ket", 3)
         load_rows("bra", 0)
         load_rows("bra", 1)
+        load_rows("bra", 2)
         load_coh(0)
         load_coh(1)
-        load_rows("bra", 2)
-        load_rows("bra", 3)
+        load_quadrants(3)
 
         order_l_scales(0, 0, 2)
         order_l_words(0, 1)
@@ -396,64 +437,71 @@ def tile_two_copy_overlap_s12_kernel(
         turn_out("ket", 3, "dve")
         rho(0, 1, 3)
         order_rows("ket", 3, "dve")
-        quant_turned("ket", 0, 0, 2 * HALF)
+        quant_ket(0)
         rho(1, 0, 0)
         weave("rho", 0, 1)
         rho(1, 0, 1)
         order_rows("bra", 0, "dve")
         order_rows("bra", 1, "dve")
         turn_run("ket", 1, ("act", "act", "act", "act"))
-        quant_woven("rho", 0, 1)
+        order_rows("bra", 2, "dve")
         rho(1, 0, 2)
-        quant_turned("ket", 1, 0, 2 * HALF)
-        turn_run("bra", 0, ("act", "act", "act", "act"))
+        quant_ket(1)
+        for j in range(6):
+            turn("bra", j, "act")
+        quant_woven("rho", 0, 1)
         quant_bra(0, 0)
         quant_bra(0, 1)
         rho(1, 0, 3)
         rho(1, 1, 0)
         weave("rho", 1, 0, 0, HALF, "act")
-        order_rows("bra", 2, "dve")
         for j in range(4):
             sig(0, 0, j)
-        order_rows("bra", 3, "dve")
+        quant_bra(1, 0)
+        weave_sig(0, 0, 0, "act")
+        weave_sig(0, 0, 1, "act")
         rho(1, 1, 1)
         quant_woven("rho", 1, 0)
-        weave_sig(0, 0, 0, HALF, "act")
-        for j in range(4):
+        order_quadrants(3, "act")
+        for j in range(2):
             sig(1, 0, j)
+        weave_sig(1, 0, 0, "act")
+        for j in range(2, 4):
+            sig(1, 0, j)
+        weave_sig(1, 0, 1, "act")
         quant_woven("sig", 0, 0)
-        weave_sig(1, 0)
-        turn_run("bra", 1, ("act", "act", "act", "act"))
+        flip(3, 0)
         rho(1, 1, 2)
-        quant_bra(1, 0)
         quant_woven("sig", 1, 0)
+        flip(3, 1)
         rho(1, 1, 3)
-        quant_bra(1, 1)
-        weave("rho", 1, 1)
+        pair_flipped(3, "act")
         sig(0, 1, 0)
-        outg("act", 0, 0, 0)
+        weave("rho", 1, 1)
         sig(0, 1, 1)
+        outg("act", 0, 0, 0)
+        quant_bra(1, 1)
         outg("act", 0, 0, 1)
+        weave_sig(0, 1, 0, "act")
         quant_woven("rho", 1, 1)
-        outg("act", 0, 0, 2)
-        weave_sig(0, 1, 0, 256, "act")
         sig(1, 1, 0)
-        outg("act", 0, 0, 3)
+        outg("act", 0, 0, 2)
         sig(1, 1, 1)
         quant_woven("sig", 0, 1, 0, 256)
-        outg("act", 1, 0, 0)
-        weave_sig(1, 1, 0, 256, "act")
+        outg("act", 0, 0, 3)
+        weave_sig(1, 1, 0, "act")
         sig(0, 1, 2)
-        outg("act", 1, 0, 1)
+        outg("act", 1, 0, 0)
         sig(0, 1, 3)
         quant_woven("sig", 1, 1, 0, 256)
+        outg("act", 1, 0, 1)
         outg("act", 1, 0, 2)
         sig(1, 1, 2)
-        weave_sig(0, 1, 256, HALF)
+        weave_sig(0, 1, 1, "dve")
         outg("act", 1, 0, 3)
         sig(1, 1, 3)
         quant_woven("sig", 0, 1, 256, HALF)
-        weave_sig(1, 1, 256, HALF)
+        weave_sig(1, 1, 1, "dve")
         quant_woven("sig", 1, 1, 256, HALF)
         for pair in range(4):
             out_quarter("act", 2, pair)

@@ -44,12 +44,14 @@ def tile_two_copy_overlap_s12_kernel(
         filt_raw = kept("filt_raw", [P, 256], BF16)
         filt_sorted = kept("filt_sorted", [P, 256], F32)
         filt_col = kept("filt_col", [P, 256], F32)
-        rows = {(w, j): kept("%s_rows%d" % (w, j), [P, 2, F], BF16) for w in ("ket", "bra") for j in range(4)}
+        rows = {(w, j): kept("%s_rows%d" % (w, j), [P, 2, F], BF16) for w, n in (("ket", 4), ("bra", 2)) for j in range(n)}
+        rows["bra", 2] = kept("bra_rows2", [P, 1, F], BF16)
+        quads = {640: kept("bra_quads640", [P, 2, 4, P], BF16), 768: kept("bra_quads768", [P, 2, 8, P], BF16)}
         turned = {("ket", g): kept("ket_turned%d" % g, [P, 2 * HALF * 4], BF16) for g in range(2)}
         for ch in range(2):
             for x in range(2):
                 turned["bra", ch, x] = kept("bra_turned%d%d" % (ch, x), [P, HALF * 4], BF16)
-        flipped = kept("flipped", [P, 2 * HALF], F32)
+        flipped = {key: kept("flipped%d_%d" % key, [P, HALF], F32) for key in ((640, 0), (768, 0), (768, 1))}
         codes = {(w, g): kept("%s_codes%d" % (w, g), [P, 2 * HALF], U32) for w in ("ket", "bra") for g in range(2)}
         scales = {(w, g): kept("%s_scales%d" % (w, g), [P, 2 * HALF], U8) for w in ("ket", "bra") for g in range(2)}
         pieces = [(0, 0, 1), (0, 1, 2), (0, 2, 4), (1, 0, 4)]
@@ -60,7 +62,7 @@ def tile_two_copy_overlap_s12_kernel(
         l_scale = [kept("l_scale%d" % g, [P, 4, 4, P], U8) for g in range(2)]
         r_words = {(h, e0): kept("r_words%d%d" % (h, e0), [P, e1 - e0, 2 * HALF], U8) for h, e0, e1 in pieces}
         r_scale = [kept("r_scale%d" % h, [P, 4, HALF], U8) for h in range(2)]
-        coh_sb = [kept("coh%d" % g, [P, 4, A], BF16) for g in range(2)]
+        coh_sb = {(g, ch): kept("coh%d%d" % (g, ch), [P, 4, HALF], BF16) for g in range(2) for ch in range(2)}
         q_codes = {(w, g, h): kept("%s_q%d%d" % (w, g, h), [P, HALF], U32) for w in ("rho", "sig") for g in range(2) for h in range(2)}
         q_scales = {(w, g, h): kept("%s_s%d%d" % (w, g, h), [P, HALF], U8) for w in ("rho", "sig") for g in range(2) for h in range(2)}
         flat = {}
@@ -68,7 +70,8 @@ def tile_two_copy_overlap_s12_kernel(
 
         def load_rows(w, j):
             src = ket if w == "ket" else bra
-            nc.sync.dma_start(out=rows[w, j][:], in_=src[2 * j * P : 2 * (j + 1) * P, :].rearrange("(s p) f -> p s f", s=2))
+            blocks = rows[w, j].shape[1]
+            nc.sync.dma_start(out=rows[w, j][:], in_=src[2 * j * P : (2 * j + blocks) * P, :].rearrange("(s p) f -> p s f", s=blocks))
 
         def load_scales(plane, src, h, r0=0, r1=4, queue=nc.sync):
             by_row = src.bitcast(I32).rearrange("e (q r) n -> r q e n", r=4)
@@ -79,10 +82,10 @@ def tile_two_copy_overlap_s12_kernel(
             view = src.bitcast(I32).rearrange("e p n -> p e n")
             nc.sync.dma_start(out=tiles[h, e0][:].bitcast(I32), in_=view[:, e0:e1, h * 256 : (h + 1) * 256])
 
-        def load_coh(g):
+        def load_coh(g, ch):
             view = coh.rearrange("(g p t j) c -> g j p t c", g=2, t=4, j=4)
             for j in range(4):
-                nc.sync.dma_start(out=coh_sb[g][j:P:4, :, :], in_=view[g][j])
+                nc.sync.dma_start(out=coh_sb[g, ch][j:P:4, :, :], in_=view[g][j][:, :, HALF * ch : HALF * (ch + 1)])
 
         def load_filt():
             nc.sync.dma_start(
@@ -109,11 +112,12 @@ def tile_two_copy_overlap_s12_kernel(
                 nc.vector.tensor_copy(out=out, in_=in_)
 
         def order_rows(w, j, engine):
-            ordered[w, j] = stage.tile([P, 2 * HALF], F32, name="ordered", bufs=4, align_bytes=64)
+            blocks = rows[w, j].shape[1]
+            ordered[w, j] = stage.tile([P, blocks * HALF], F32, name="ordered", bufs=4, align_bytes=64)
             copy_on(
                 engine,
-                ordered[w, j][:].rearrange("k (x u q i) -> k x u q i", x=4, u=2, i=8),
-                rows[w, j][:].rearrange("k s f -> k (s f)").bitcast(F32).rearrange("k (x q u i) -> k x u q i", x=4, u=2, i=8),
+                ordered[w, j][:].rearrange("k (x u q i) -> k x u q i", u=2, q=16, i=8),
+                rows[w, j][:].rearrange("k s f -> k (s f)").bitcast(F32).rearrange("k (x q u i) -> k x u q i", u=2, q=16, i=8),
             )
 
         def turn_mm(w, j):
@@ -146,47 +150,36 @@ def tile_two_copy_overlap_s12_kernel(
         def quant_ket(g):
             nc.vector.quantize_mx(out=codes["ket", g][:].bitcast(FP8X4), scales=scales["ket", g][:], in_=turned["ket", g][:])
 
-        def quant_bra(ch, x):
-            cols = slice(HALF * x, HALF * (x + 1))
-            nc.vector.quantize_mx(out=codes["bra", ch][:, cols].bitcast(FP8X4), scales=scales["bra", ch][:, cols], in_=turned["bra", ch, x][:])
+        def quant_bra(ch, x, c0=0, c1=HALF):
+            cols = slice(HALF * x + c0, HALF * x + c1)
+            nc.vector.quantize_mx(
+                out=codes["bra", ch][:, cols].bitcast(FP8X4), scales=scales["bra", ch][:, cols], in_=turned["bra", ch, x][:, 4 * c0 : 4 * c1]
+            )
 
-        def load_quadrants(j):
-            src = bra[2 * j * P : 2 * (j + 1) * P, :].rearrange("(b r) (h q f) -> h q r b f", r=32, h=2, q=4)
-            dst = rows["bra", j][:].rearrange("k h (b f) -> k h b f", b=8)
+        def load_quadrants(c0):
+            blocks = quads[c0].shape[2]
+            src = bra[c0 : c0 + 32 * blocks, :].rearrange("(b r) (h q f) -> h q r b f", r=32, h=2, q=4)
             for h in range(2):
                 for q in range(4):
-                    nc.sync.dma_start(out=dst[32 * q : 32 * (q + 1), h], in_=src[h][q])
+                    nc.sync.dma_start(out=quads[c0][32 * q : 32 * (q + 1), h], in_=src[h][q])
 
-        def order_quadrants(j, engine):
-            ordered["bra", j] = stage.tile([P, 2 * HALF], F32, name="ordered", bufs=4, align_bytes=64)
-            src = rows["bra", j][:].rearrange("k h f -> k (h f)")
-            if engine == "act":
-                nc.scalar.copy(
-                    out=ordered["bra", j][:].bitcast(BF16).rearrange("k (x u q i) -> k x u q i", u=2, q=4, i=16),
-                    in_=src.rearrange("k (x q u i) -> k x u q i", u=2, q=4, i=16),
-                )
-            else:
-                nc.vector.tensor_copy(
-                    out=ordered["bra", j][:].rearrange("k (x u q i) -> k x u q i", u=2, q=4, i=8),
-                    in_=src.bitcast(F32).rearrange("k (x q u i) -> k x u q i", u=2, q=4, i=8),
-                )
+        def order_quadrants(c0, h0, h1):
+            ordered["bra", c0, h0] = stage.tile([P, HALF], F32, name="ordered", bufs=4, align_bytes=64)
+            nc.scalar.copy(
+                out=ordered["bra", c0, h0][:].bitcast(BF16).rearrange("k (x u q i) -> k x u q i", u=2, q=4, i=16),
+                in_=quads[c0][:, h0:h1].rearrange("k h b (q u i) -> k (h b) u q i", u=2, q=4, i=16),
+            )
 
-        def flip(j, h):
-            cols = slice(HALF * h, HALF * (h + 1))
-            nc.vector.transpose(out=flipped[:, cols], in_=ordered["bra", j][:, cols])
+        def flip(c0, h0):
+            nc.vector.transpose(out=flipped[c0, h0][:], in_=ordered["bra", c0, h0][:])
 
-        def pair_flipped(j, engine):
-            dst = turned["bra", j // 2, j % 2][:]
-            if engine == "act":
-                nc.scalar.copy(
-                    out=dst.rearrange("p (x r u e) -> p x r u e", r=32, u=2, e=2),
-                    in_=flipped[:].bitcast(BF16).rearrange("p (x u r e) -> p x r u e", r=32, u=2, e=2),
-                )
-            else:
-                nc.vector.tensor_copy(
-                    out=dst.bitcast(F32).rearrange("p (x r u) -> p x r u", r=32, u=2),
-                    in_=flipped[:].rearrange("p (x u r) -> p x r u", r=32, u=2),
-                )
+        def pair_flipped(c0, h0, h):
+            blocks = quads[c0].shape[2]
+            dst = turned["bra", 1, c0 // 768][:].rearrange("p (h c x) -> p h c x", h=2, x=4)[:, h, c0 % 256 : c0 % 256 + 32 * blocks]
+            nc.scalar.copy(
+                out=dst.rearrange("p (b r) (u e) -> p b r u e", r=32, e=2),
+                in_=flipped[c0, h0][:].bitcast(BF16).rearrange("p (h b u r e) -> p h b r u e", b=blocks, r=32, u=2, e=2)[:, h - h0],
+            )
 
         def order_l_scales(g, e0=0, e1=4):
             nc.vector.tensor_copy(
@@ -266,11 +259,10 @@ def tile_two_copy_overlap_s12_kernel(
             cq, tp = jj // 2, jj % 2
             if tp == 0:
                 paired[g, ch, cq] = stage.tile([P, 2, 256, 2], BF16, name="paired", bufs=5, align_bytes=64)
-            col0 = HALF * ch + 256 * cq
             nc.vector.tensor_tensor(
                 out=paired[g, ch, cq][:, tp],
                 in0=held["sig", g, ch, jj][:].rearrange("p (t c) -> p c t", t=2),
-                in1=coh_sb[g][:, 2 * tp : 2 * tp + 2, col0 : col0 + 256].rearrange("p t c -> p c t"),
+                in1=coh_sb[g, ch][:, 2 * tp : 2 * tp + 2, 256 * cq : 256 * (cq + 1)].rearrange("p t c -> p c t"),
                 op=MULT,
             )
 
@@ -326,18 +318,18 @@ def tile_two_copy_overlap_s12_kernel(
         def out_quarter(engine, cq, pair):
             bank = next_bank()
             c_cols = slice(256 * (cq % 2), 256 * (cq % 2 + 1))
-            for s in range(2):
-                ah, i = divmod(2 * pair + s, 4)
-                a_cols = slice(P * i, P * (i + 1))
-                for g in range(2):
+            for g in range(2):
+                for s in range(2):
+                    ah, i = divmod(2 * pair + s, 4)
+                    a_cols = slice(P * i, P * (i + 1))
                     nc.tensor.matmul_mx(
                         out=bank[:, 256 * s : 256 * (s + 1)],
                         lhsT=q_codes["rho", g, ah][:, a_cols].bitcast(FP8X4),
                         lhsT_scale=q_scales["rho", g, ah][:, a_cols],
                         rhs=q_codes["sig", g, cq // 2][:, c_cols].bitcast(FP8X4),
                         rhs_scale=q_scales["sig", g, cq // 2][:, c_cols],
-                        start=(g == 0),
-                        stop=(g == 1),
+                        start=(g == 0 and s == 0),
+                        stop=(g == 1 and s == 1),
                     )
             result = stage.tile([P, HALF], F32, name="result", bufs=8, align_bytes=64)
             copy_on(engine, result[:], bank[:])
@@ -397,9 +389,12 @@ def tile_two_copy_overlap_s12_kernel(
         load_rows("bra", 0)
         load_rows("bra", 1)
         load_rows("bra", 2)
-        load_coh(0)
-        load_coh(1)
-        load_quadrants(3)
+        load_coh(0, 0)
+        load_coh(1, 0)
+        load_quadrants(640)
+        load_quadrants(768)
+        load_coh(0, 1)
+        load_coh(1, 1)
 
         order_l_scales(0, 0, 2)
         order_l_words(0, 1)
@@ -447,40 +442,49 @@ def tile_two_copy_overlap_s12_kernel(
         order_rows("bra", 2, "dve")
         rho(1, 0, 2)
         quant_ket(1)
-        for j in range(6):
+        for j in range(5):
             turn("bra", j, "act")
         quant_woven("rho", 0, 1)
         quant_bra(0, 0)
         quant_bra(0, 1)
+        for h in range(2):
+            quant_bra(1, 0, 256 * h, 256 * h + P)
         rho(1, 0, 3)
         rho(1, 1, 0)
+        order_quadrants(640, 0, 2)
         weave("rho", 1, 0, 0, HALF, "act")
         for j in range(4):
             sig(0, 0, j)
-        quant_bra(1, 0)
         weave_sig(0, 0, 0, "act")
         weave_sig(0, 0, 1, "act")
-        rho(1, 1, 1)
+        flip(640, 0)
         quant_woven("rho", 1, 0)
-        order_quadrants(3, "act")
+        rho(1, 1, 1)
+        pair_flipped(640, 0, 0)
+        pair_flipped(640, 0, 1)
         for j in range(2):
             sig(1, 0, j)
         weave_sig(1, 0, 0, "act")
+        order_quadrants(768, 0, 1)
         for j in range(2, 4):
             sig(1, 0, j)
         weave_sig(1, 0, 1, "act")
+        order_quadrants(768, 1, 2)
+        for h in range(2):
+            quant_bra(1, 0, 256 * h + P, 256 * (h + 1))
         quant_woven("sig", 0, 0)
-        flip(3, 0)
+        flip(768, 0)
         rho(1, 1, 2)
         quant_woven("sig", 1, 0)
-        flip(3, 1)
+        flip(768, 1)
         rho(1, 1, 3)
-        pair_flipped(3, "act")
+        pair_flipped(768, 0, 0)
+        pair_flipped(768, 1, 1)
         sig(0, 1, 0)
         weave("rho", 1, 1)
+        quant_bra(1, 1)
         sig(0, 1, 1)
         outg("act", 0, 0, 0)
-        quant_bra(1, 1)
         outg("act", 0, 0, 1)
         weave_sig(0, 1, 0, "act")
         quant_woven("rho", 1, 1)

from contextlib import ExitStack

import concourse.mybir as mybir
from concourse.masks import make_identity

F32 = mybir.dt.float32
BF16 = mybir.dt.bfloat16
I32 = mybir.dt.int32
U32 = mybir.dt.uint32
U8 = mybir.dt.uint8
FP8X4 = mybir.dt.float8_e4m3fn_x4
FP4X4 = mybir.dt.float4_e2m1fn_x4
MULT = mybir.AluOpType.mult
COPY = mybir.ActivationFunctionType.Copy

A, E, F = 1024, 2048, 1024
FLOPS = 2 * A * A * (E + F + A)
P = 128
HALF = 512


def tile_two_copy_overlap_s12_kernel(
    tc, ref_ket_words, ref_ket_scales, ref_bra_words, ref_bra_scales, ket, bra, filt, coh, out
):
    nc = tc.nc
    with ExitStack() as ctx:
        keep = ctx.enter_context(tc.tile_pool(name="keep", bufs=1))
        stage = ctx.enter_context(tc.tile_pool(name="stage", bufs=2))
        psum = ctx.enter_context(tc.psum_pool(name="psum", bufs=1))
        ctx.enter_context(tc.manual_schedule())

        def kept(name, shape, dtype):
            return keep.tile(shape, dtype, name=name, align_bytes=64)

        banks = [psum.tile([P, HALF], F32, name="bank%d" % b) for b in range(8)]
        used = [0]

        def next_bank():
            used[0] += 1
            return banks[(used[0] - 1) % 8]

        ident = kept("ident", [P, P], F32)
        perm = kept("perm", [P, P], F32)
        filt_raw = kept("filt_raw", [P, 256], BF16)
        filt_sorted = kept("filt_sorted", [P, 256], F32)
        filt_col = kept("filt_col", [P, 256], F32)
        rows = {(w, j): kept("%s_rows%d" % (w, j), [P, 2, F], BF16) for w, n in (("ket", 4), ("bra", 2)) for j in range(n)}
        rows["bra", 2] = kept("bra_rows2", [P, 1, F], BF16)
        quads = {640: kept("bra_quads640", [P, 2, 4, P], BF16), 768: kept("bra_quads768", [P, 2, 8, P], BF16)}
        turned = {("ket", g): kept("ket_turned%d" % g, [P, 2 * HALF * 4], BF16) for g in range(2)}
        for ch in range(2):
            for x in range(2):
                turned["bra", ch, x] = kept("bra_turned%d%d" % (ch, x), [P, HALF * 4], BF16)
        flipped = {key: kept("flipped%d_%d" % key, [P, HALF], F32) for key in ((640, 0), (768, 0), (768, 1))}
        codes = {(w, g): kept("%s_codes%d" % (w, g), [P, 2 * HALF], U32) for w in ("ket", "bra") for g in range(2)}
        scales = {(w, g): kept("%s_scales%d" % (w, g), [P, 2 * HALF], U8) for w in ("ket", "bra") for g in range(2)}
        pieces = [(0, 0, 1), (0, 1, 2), (0, 2, 4), (1, 0, 4)]
        first_pass = {(h, e): e0 for h, e0, e1 in pieces for e in range(e0, e1)}
        l_raw = {(g, e0): kept("l_raw%d%d" % (g, e0), [P, e1 - e0, 2 * HALF], U8) for g, e0, e1 in pieces}
        l_words = {(g, e0): kept("l_words%d%d" % (g, e0), [P, 4, e1 - e0, 2 * P], U8) for g, e0, e1 in pieces}
        l_scale_raw = [kept("l_scale_raw%d" % g, [P, 4, HALF], U8) for g in range(2)]
        l_scale = [kept("l_scale%d" % g, [P, 4, 4, P], U8) for g in range(2)]
        r_words = {(h, e0): kept("r_words%d%d" % (h, e0), [P, e1 - e0, 2 * HALF], U8) for h, e0, e1 in pieces}
        r_scale = [kept("r_scale%d" % h, [P, 4, HALF], U8) for h in range(2)]
        coh_sb = {(g, ch): kept("coh%d%d" % (g, ch), [P, 4, HALF], BF16) for g in range(2) for ch in range(2)}
        q_codes = {(w, g, h): kept("%s_q%d%d" % (w, g, h), [P, HALF], U32) for w in ("rho", "sig") for g in range(2) for h in range(2)}
        q_scales = {(w, g, h): kept("%s_s%d%d" % (w, g, h), [P, HALF], U8) for w in ("rho", "sig") for g in range(2) for h in range(2)}
        flat = {}
        woven = {}

        def load_rows(w, j):
            src = ket if w == "ket" else bra
            blocks = rows[w, j].shape[1]
            nc.sync.dma_start(out=rows[w, j][:], in_=src[2 * j * P : (2 * j + blocks) * P, :].rearrange("(s p) f -> p s f", s=blocks))

        def load_scales(plane, src, h, r0=0, r1=4, queue=nc.sync):
            by_row = src.bitcast(I32).rearrange("e (q r) n -> r q e n", r=4)
            for r in range(r0, r1):
                queue.dma_start(out=plane[r:P:32, :, :].bitcast(I32), in_=by_row[r][:, :, h * P : (h + 1) * P])

        def load_words(tiles, src, h, e0, e1):
            view = src.bitcast(I32).rearrange("e p n -> p e n")
            nc.sync.dma_start(out=tiles[h, e0][:].bitcast(I32), in_=view[:, e0:e1, h * 256 : (h + 1) * 256])

        def load_coh(g, ch):
            view = coh.rearrange("(g p t j) c -> g j p t c", g=2, t=4, j=4)
            for j in range(4):
                nc.sync.dma_start(out=coh_sb[g, ch][j:P:4, :, :], in_=view[g][j][:, :, HALF * ch : HALF * (ch + 1)])

        def load_filt():
            nc.sync.dma_start(
                out=filt_raw[0:P:32, :].rearrange("q (g n) -> q g n", g=2), in_=filt.rearrange("(g q n) -> q g n", g=2, q=4)
            )

        def spread_filt():
            nc.vector.tensor_copy(
                out=filt_sorted[:].rearrange("q (g t x j) -> q g t x j", g=2, t=4, j=4),
                in_=filt_raw[:].rearrange("q (g x t j) -> q g t x j", g=2, t=4, j=4),
            )
            nc.vector.transpose(out=filt_col[:], in_=filt_sorted[:])

        def zero(engine, plane):
            engine.memset(plane[:].rearrange("p e n -> p (e n)").bitcast(I32), 0)

        ordered = {}
        turned_bank = {}

        def copy_on(engine, out, in_):
            if engine == "act":
                nc.scalar.copy(out=out, in_=in_)
            else:
                nc.vector.tensor_copy(out=out, in_=in_)

        def order_rows(w, j, engine):
            blocks = rows[w, j].shape[1]
            ordered[w, j] = stage.tile([P, blocks * HALF], F32, name="ordered", bufs=4, align_bytes=64)
            copy_on(
                engine,
                ordered[w, j][:].rearrange("k (x u q i) -> k x u q i", u=2, q=16, i=8),
                rows[w, j][:].rearrange("k s f -> k (s f)").bitcast(F32).rearrange("k (x q u i) -> k x u q i", u=2, q=16, i=8),
            )

        def turn_mm(w, j):
            bank = next_bank()
            turned_bank[w, j] = bank
            for u in range(2):
                for h in range(2):
                    w0 = HALF * (j % 2) + 256 * h + P * u
                    src = ordered[w, j // 2][:, w0 : w0 + P]
                    nc.tensor.transpose(
                        bank[:, 256 * u + P * h : 256 * u + P * (h + 1)], src, (perm if w == "ket" else ident)[:]
                    )

        def turn_out(w, j, engine):
            bank = turned_bank[w, j]
            jj = j % 4
            if w == "ket":
                copy_on(
                    engine,
                    turned[w, j // 4][:].bitcast(F32).rearrange("p (s jj c u) -> p jj s c u", s=8, jj=4, u=2)[:, jj],
                    bank[:].rearrange("p (u s c) -> p s c u", u=2, s=8),
                )
            else:
                copy_on(
                    engine,
                    turned[w, j // 4, jj // 2][:].bitcast(F32).rearrange("p (h j2 c u) -> p j2 h c u", h=2, j2=2, u=2)[:, jj % 2],
                    bank[:].rearrange("p (u h c) -> p h c u", u=2, h=2),
                )

        def quant_ket(g):
            nc.vector.quantize_mx(out=codes["ket", g][:].bitcast(FP8X4), scales=scales["ket", g][:], in_=turned["ket", g][:])

        def quant_bra(ch, x, c0=0, c1=HALF):
            cols = slice(HALF * x + c0, HALF * x + c1)
            nc.vector.quantize_mx(
                out=codes["bra", ch][:, cols].bitcast(FP8X4), scales=scales["bra", ch][:, cols], in_=turned["bra", ch, x][:, 4 * c0 : 4 * c1]
            )

        def load_quadrants(c0):
            blocks = quads[c0].shape[2]
            src = bra[c0 : c0 + 32 * blocks, :].rearrange("(b r) (h q f) -> h q r b f", r=32, h=2, q=4)
            for h in range(2):
                for q in range(4):
                    nc.sync.dma_start(out=quads[c0][32 * q : 32 * (q + 1), h], in_=src[h][q])

        def order_quadrants(c0, h0, h1):
            ordered["bra", c0, h0] = stage.tile([P, HALF], F32, name="ordered", bufs=4, align_bytes=64)
            nc.scalar.copy(
                out=ordered["bra", c0, h0][:].bitcast(BF16).rearrange("k (x u q i) -> k x u q i", u=2, q=4, i=16),
                in_=quads[c0][:, h0:h1].rearrange("k h b (q u i) -> k (h b) u q i", u=2, q=4, i=16),
            )

        def flip(c0, h0):
            nc.vector.transpose(out=flipped[c0, h0][:], in_=ordered["bra", c0, h0][:])

        def pair_flipped(c0, h0, h):
            blocks = quads[c0].shape[2]
            dst = turned["bra", 1, c0 // 768][:].rearrange("p (h c x) -> p h c x", h=2, x=4)[:, h, c0 % 256 : c0 % 256 + 32 * blocks]
            nc.scalar.copy(
                out=dst.rearrange("p (b r) (u e) -> p b r u e", r=32, e=2),
                in_=flipped[c0, h0][:].bitcast(BF16).rearrange("p (h b u r e) -> p h b r u e", b=blocks, r=32, u=2, e=2)[:, h - h0],
            )

        def order_l_scales(g, e0=0, e1=4):
            nc.vector.tensor_copy(
                out=l_scale[g][:, :, e0:e1, :].rearrange("k t e n -> k t (e n)").bitcast(I32).rearrange("k t (b i) -> k b t i", i=4),
                in_=l_scale_raw[g][:, e0:e1, :].rearrange("k e n -> k (e n)").bitcast(I32).rearrange("k (b i t) -> k b t i", i=4, t=4),
            )

        def order_l_words(g, e0):
            nc.vector.tensor_copy(
                out=l_words[g, e0][:].rearrange("k t e n -> k t (e n)").bitcast(I32).rearrange("k t (x w) -> k t x w", w=2),
                in_=l_raw[g, e0][:].rearrange("k e n -> k (e n)").bitcast(I32).rearrange("k (x t w) -> k t x w", t=4, w=2),
            )

        def rho_pass(bank, g, ah, t, e):
            nc.tensor.matmul_mx(
                out=bank[:],
                lhsT=l_words[g, first_pass[g, e]][:, t, e - first_pass[g, e], :].bitcast(FP4X4),
                lhsT_scale=l_scale[g][:, t, e, :],
                rhs=r_words[ah, first_pass[ah, e]][:, e - first_pass[ah, e], :].bitcast(FP4X4),
                rhs_scale=r_scale[ah][:, e, :],
                start=(e == 0),
                stop=(e == 3),
            )

        held = {}

        def rho_mm(g, ah, t):
            held["rho", g, ah, t] = next_bank()
            for e in range(4):
                rho_pass(held["rho", g, ah, t], g, ah, t, e)

        def rho_out(g, ah, t, c0=0, c1=HALF):
            bank = held["rho", g, ah, t]
            if t == 0:
                flat["rho", g, ah] = stage.tile([P, 4, HALF], BF16, name="rho_flat", bufs=3, align_bytes=64)
            nc.scalar.activation(out=flat["rho", g, ah][:, t, c0:c1], in_=bank[:, c0:c1], func=COPY, scale=filt_col[:, 32 * (4 * g + t) : 32 * (4 * g + t) + 1])

        def weave(w, g, ah, c0=0, c1=HALF, engine="dve"):
            if c0 == 0:
                woven[w, g, ah] = stage.tile([P, HALF * 4], BF16, name="woven", bufs=4, align_bytes=64)
            copy_on(
                engine,
                woven[w, g, ah][:, 4 * c0 : 4 * c1].rearrange("p (c i t) -> p c t i", i=4, t=4),
                flat[w, g, ah][:, :, c0:c1].rearrange("p t (c i) -> p c t i", i=4),
            )

        def quant_woven(w, g, h, c0=0, c1=HALF):
            nc.vector.quantize_mx(
                out=q_codes[w, g, h][:, c0:c1].bitcast(FP8X4),
                scales=q_scales[w, g, h][:, c0:c1],
                in_=woven[w, g, h][:, 4 * c0 : 4 * c1],
            )

        paired = {}
        woven_sig = {}

        def sig_mm(g, ch, jj):
            bank = next_bank()
            held["sig", g, ch, jj] = bank
            cq, tp = jj // 2, jj % 2
            for t2 in range(2):
                for h in range(2):
                    m0 = HALF * h + P * (2 * tp + t2)
                    m_cols = slice(m0, m0 + P)
                    cols = slice(HALF * cq + 256 * h, HALF * cq + 256 * (h + 1))
                    nc.tensor.matmul_mx(
                        out=bank[:, 256 * t2 : 256 * (t2 + 1)],
                        lhsT=codes["ket", g][:, m_cols].bitcast(FP8X4),
                        lhsT_scale=scales["ket", g][:, m_cols],
                        rhs=codes["bra", ch][:, cols].bitcast(FP8X4),
                        rhs_scale=scales["bra", ch][:, cols],
                        start=(h == 0),
                        stop=(h == 1),
                    )

        def sig_out(g, ch, jj):
            cq, tp = jj // 2, jj % 2
            if tp == 0:
                paired[g, ch, cq] = stage.tile([P, 2, 256, 2], BF16, name="paired", bufs=5, align_bytes=64)
            nc.vector.tensor_tensor(
                out=paired[g, ch, cq][:, tp],
                in0=held["sig", g, ch, jj][:].rearrange("p (t c) -> p c t", t=2),
                in1=coh_sb[g, ch][:, 2 * tp : 2 * tp + 2, 256 * cq : 256 * (cq + 1)].rearrange("p t c -> p c t"),
                op=MULT,
            )

        def weave_sig(g, ch, cq, engine):
            if (g, ch) not in woven_sig:
                woven_sig[g, ch] = stage.tile([P, HALF * 4], BF16, name="woven", bufs=4, align_bytes=64)
                woven["sig", g, ch] = woven_sig[g, ch]
            dst = woven_sig[g, ch][:, 1024 * cq : 1024 * (cq + 1)]
            if engine == "act":
                nc.scalar.copy(
                    out=dst.rearrange("p (c tp t) -> p c tp t", tp=2, t=2),
                    in_=paired[g, ch, cq][:].rearrange("p tp c t -> p c tp t"),
                )
            else:
                nc.vector.tensor_copy(
                    out=dst.bitcast(F32).rearrange("p (c tp) -> p c tp", tp=2),
                    in_=paired[g, ch, cq][:].rearrange("p tp c t -> p tp (c t)").bitcast(F32).rearrange("p tp c -> p c tp"),
                )

        def warm_up(count, plane):
            for i in range(count):
                nc.tensor.matmul_mx(
                    out=banks[7][:],
                    lhsT=l_raw[0, 0][:, 0, 0 : 2 * P].bitcast(FP4X4),
                    lhsT_scale=plane[:, 0, 0:P],
                    rhs=l_raw[0, 0][:, 0, :].bitcast(FP4X4),
                    rhs_scale=plane[:, 0, :],
                    start=True,
                    stop=True,
                )

        def out_mm(ah, ch, i, c0=0, c1=HALF):
            bank = next_bank()
            held["out", ah, ch, i, c0] = bank
            a_cols = slice(P * i, P * (i + 1))
            for g in range(2):
                nc.tensor.matmul_mx(
                    out=bank[:, 0 : c1 - c0],
                    lhsT=q_codes["rho", g, ah][:, a_cols].bitcast(FP8X4),
                    lhsT_scale=q_scales["rho", g, ah][:, a_cols],
                    rhs=q_codes["sig", g, ch][:, c0:c1].bitcast(FP8X4),
                    rhs_scale=q_scales["sig", g, ch][:, c0:c1],
                    start=(g == 0),
                    stop=(g == 1),
                )

        def out_store(engine, ah, ch, i, c0=0, c1=HALF):
            result = stage.tile([P, c1 - c0], F32, name="result", bufs=8, align_bytes=64)
            copy_on(engine, result[:], held["out", ah, ch, i, c0][:, 0 : c1 - c0])
            row0 = HALF * ah + P * i
            nc.sync.dma_start(out=out[row0 : row0 + P, HALF * ch + c0 : HALF * ch + c1], in_=result[:])

        def out_quarter(engine, cq, pair):
            bank = next_bank()
            c_cols = slice(256 * (cq % 2), 256 * (cq % 2 + 1))
            for g in range(2):
                for s in range(2):
                    ah, i = divmod(2 * pair + s, 4)
                    a_cols = slice(P * i, P * (i + 1))
                    nc.tensor.matmul_mx(
                        out=bank[:, 256 * s : 256 * (s + 1)],
                        lhsT=q_codes["rho", g, ah][:, a_cols].bitcast(FP8X4),
                        lhsT_scale=q_scales["rho", g, ah][:, a_cols],
                        rhs=q_codes["sig", g, cq // 2][:, c_cols].bitcast(FP8X4),
                        rhs_scale=q_scales["sig", g, cq // 2][:, c_cols],
                        start=(g == 0 and s == 0),
                        stop=(g == 1 and s == 1),
                    )
            result = stage.tile([P, HALF], F32, name="result", bufs=8, align_bytes=64)
            copy_on(engine, result[:], bank[:])
            nc.sync.dma_start(
                out=out[2 * P * pair : 2 * P * (pair + 1), 256 * cq : 256 * (cq + 1)].rearrange("(s p) c -> p s c", s=2),
                in_=result[:].rearrange("p (s c) -> p s c", s=2),
            )

        def rho(g, ah, t):
            rho_mm(g, ah, t)
            rho_out(g, ah, t)

        def sig(g, ch, t):
            sig_mm(g, ch, t)
            sig_out(g, ch, t)

        def turn(w, j, engine):
            turn_mm(w, j)
            turn_out(w, j, engine)

        def outg(engine, ah, ch, i, c0=0, c1=HALF):
            out_mm(ah, ch, i, c0, c1)
            out_store(engine, ah, ch, i, c0, c1)

        load_words(l_raw, ref_bra_words, 0, 0, 1)
        load_words(r_words, ref_ket_words, 0, 0, 1)
        zero(nc.vector, r_scale[0])
        zero(nc.vector, l_scale_raw[0])
        zero(nc.vector, l_scale_raw[1])
        load_scales(r_scale[0], ref_ket_scales, 0, 0, 2)
        load_scales(l_scale_raw[0], ref_bra_scales, 0)
        load_scales(r_scale[0], ref_ket_scales, 0, 2, 3)
        load_scales(r_scale[0], ref_ket_scales, 0, 3, 4, nc.gpsimd)
        nc.vector.memset(ident[:], 0.0)
        make_identity(nc, ident[:], nomemset=True)
        nc.scalar.activation(
            out=perm[:].rearrange("k (t p j) -> k t p j", t=4, j=4), in_=ident[:].rearrange("k (p t j) -> k t p j", t=4, j=4), func=COPY
        )
        warm_up(3, l_scale_raw[1])
        warm_up(1, l_scale_raw[0])
        order_l_words(0, 0)
        zero(nc.vector, r_scale[1])
        nc.vector.memset(filt_raw[:], 0.0)
        load_words(l_raw, ref_bra_words, 0, 1, 2)
        load_words(r_words, ref_ket_words, 0, 1, 2)
        load_words(l_raw, ref_bra_words, 0, 2, 4)
        load_words(r_words, ref_ket_words, 0, 2, 4)
        load_filt()
        load_scales(r_scale[1], ref_ket_scales, 1)
        load_words(r_words, ref_ket_words, 1, 0, 4)
        load_rows("ket", 0)
        load_rows("ket", 1)
        load_scales(l_scale_raw[1], ref_bra_scales, 1)
        load_words(l_raw, ref_bra_words, 1, 0, 4)
        load_rows("ket", 2)
        load_rows("ket", 3)
        load_rows("bra", 0)
        load_rows("bra", 1)
        load_rows("bra", 2)
        load_coh(0, 0)
        load_coh(1, 0)
        load_quadrants(640)
        load_quadrants(768)
        load_coh(0, 1)
        load_coh(1, 1)

        order_l_scales(0, 0, 2)
        order_l_words(0, 1)
        order_l_scales(0, 2, 4)
        order_l_words(0, 2)
        spread_filt()

        def turn_run(w, half, engines):
            for j in range(4):
                turn(w, 4 * half + j, engines[j])

        for t in range(4):
            held["rho", 0, 0, t] = next_bank()
        for e in range(2):
            for t in range(4):
                rho_pass(held["rho", 0, 0, t], 0, 0, t, e)
        for t in range(4):
            for e in range(2, 4):
                rho_pass(held["rho", 0, 0, t], 0, 0, t, e)
            rho_out(0, 0, t)
        rho(0, 1, 0)
        order_rows("ket", 0, "dve")
        weave("rho", 0, 0)
        rho(0, 1, 1)
        order_rows("ket", 1, "dve")
        rho(0, 1, 2)
        order_l_scales(1)
        quant_woven("rho", 0, 0)
        order_l_words(1, 0)
        for j in range(4):
            turn_mm("ket", j)
        for j in range(3):
            turn_out("ket", j, "act")
        order_rows("ket", 2, "dve")
        turn_out("ket", 3, "dve")
        rho(0, 1, 3)
        order_rows("ket", 3, "dve")
        quant_ket(0)
        rho(1, 0, 0)
        weave("rho", 0, 1)
        rho(1, 0, 1)
        order_rows("bra", 0, "dve")
        order_rows("bra", 1, "dve")
        turn_run("ket", 1, ("act", "act", "act", "act"))
        order_rows("bra", 2, "dve")
        rho(1, 0, 2)
        quant_ket(1)
        for j in range(5):
            turn("bra", j, "act")
        quant_woven("rho", 0, 1)
        quant_bra(0, 0)
        quant_bra(0, 1)
        for h in range(2):
            quant_bra(1, 0, 256 * h, 256 * h + P)
        rho(1, 0, 3)
        rho(1, 1, 0)
        order_quadrants(640, 0, 2)
        weave("rho", 1, 0, 0, HALF, "act")
        for j in range(4):
            sig(0, 0, j)
        weave_sig(0, 0, 0, "act")
        weave_sig(0, 0, 1, "act")
        flip(640, 0)
        quant_woven("rho", 1, 0)
        rho(1, 1, 1)
        pair_flipped(640, 0, 0)
        pair_flipped(640, 0, 1)
        for j in range(2):
            sig(1, 0, j)
        weave_sig(1, 0, 0, "act")
        order_quadrants(768, 0, 1)
        for j in range(2, 4):
            sig(1, 0, j)
        weave_sig(1, 0, 1, "act")
        order_quadrants(768, 1, 2)
        for h in range(2):
            quant_bra(1, 0, 256 * h + P, 256 * (h + 1))
        quant_woven("sig", 0, 0)
        flip(768, 0)
        rho(1, 1, 2)
        quant_woven("sig", 1, 0)
        flip(768, 1)
        rho(1, 1, 3)
        pair_flipped(768, 0, 0)
        pair_flipped(768, 1, 1)
        sig(0, 1, 0)
        weave("rho", 1, 1)
        quant_bra(1, 1)
        sig(0, 1, 1)
        outg("act", 0, 0, 0)
        outg("act", 0, 0, 1)
        weave_sig(0, 1, 0, "act")
        quant_woven("rho", 1, 1)
        sig(1, 1, 0)
        outg("act", 0, 0, 2)
        sig(1, 1, 1)
        quant_woven("sig", 0, 1, 0, 256)
        outg("act", 0, 0, 3)
        weave_sig(1, 1, 0, "act")
        sig(0, 1, 2)
        outg("act", 1, 0, 0)
        sig(0, 1, 3)
        quant_woven("sig", 1, 1, 0, 256)
        outg("act", 1, 0, 1)
        outg("act", 1, 0, 2)
        sig(1, 1, 2)
        weave_sig(0, 1, 1, "dve")
        outg("act", 1, 0, 3)
        sig(1, 1, 3)
        quant_woven("sig", 0, 1, 256, HALF)
        weave_sig(1, 1, 1, "dve")
        quant_woven("sig", 1, 1, 256, HALF)
        for pair in range(4):
            out_quarter("act", 2, pair)
        for pair in range(3):
            out_quarter("dve" if pair % 2 == 0 else "act", 3, pair)
        outg("act", 1, 1, 2, 256, HALF)
        outg("dve", 1, 1, 3, 256, HALF)
